import numpy as np
import ml_dtypes


def mxq(x, axis, fmt="e4m3"):
    dtype, down = {"e4m3": (ml_dtypes.float8_e4m3fn, 7), "e5m2": (ml_dtypes.float8_e5m2, 14)}[fmt]
    v = np.moveaxis(np.asarray(x, np.float32).astype(ml_dtypes.bfloat16).astype(np.float64), axis, -1)
    blocks = v.reshape(v.shape[:-1] + (-1, 32))
    amax = np.abs(blocks).max(-1, keepdims=True)
    byte = np.maximum(np.where(amax > 0, np.frexp(amax)[1] - 1 + 127, 0) - down, 1)
    scale = np.exp2(byte - 127.0)
    codes = (blocks / scale).astype(np.float32).astype(dtype).astype(np.float64)
    return np.moveaxis((codes * scale).reshape(v.shape), -1, axis)


WIDE = False


def mx_kscale(k):
    if not WIDE:
        return np.ones(k)
    levels = np.array([10, -10, 5, -5, 0])
    if k % 512:
        return np.exp2(np.random.permutation(np.resize(levels, k // 32))).repeat(32)
    a = np.empty((k // 512, 16))
    for p in range(k // 512):
        a[p, :8] = np.random.permutation(np.resize(levels, 8))
        for g in range(8):
            far = levels[np.abs(levels - a[p, g]) >= 10]
            a[p, g + 8] = far[np.random.randint(len(far))]
    return np.exp2(a.ravel()).repeat(32)


def f64(x):
    return np.asarray(x).astype(np.float64)


def striped(idx):
    return np.tile(idx.reshape(-1, 16).T, (8, 1)).astype(np.uint16)


def unstriped(offs):
    return offs[:16].T.reshape(-1).astype(np.int64)


def pack_weight(w):
    k, n = w.shape
    w = f64(np.asarray(w, np.float32).astype(ml_dtypes.bfloat16)).reshape(k // 32, 32, n)
    amax = np.abs(w).max(1)
    byte = np.clip(np.where(amax > 0, np.frexp(amax)[1] - 1 + 127 - 7, 1), 1, 254)
    scaled = (w * np.exp2(127.0 - byte)[:, None, :]).reshape(k, n).astype(np.float32)
    words = np.ascontiguousarray(scaled.reshape(k // 512, 128, 4, n).transpose(0, 1, 3, 2)).astype(ml_dtypes.float8_e4m3fn).view(np.uint8)
    return words, np.ascontiguousarray(byte.astype(np.uint8).reshape(k // 512, 16, n))


def unpack_weight(words, scales):
    g, p, n, _ = words.shape
    vals = np.ascontiguousarray(words).view(ml_dtypes.float8_e4m3fn).astype(np.float64) * np.repeat(np.exp2(scales.astype(np.float64) - 127.0), 8, axis=1)[..., None]
    return vals.transpose(0, 1, 3, 2).reshape(g * 512, n)


K, T, S, V, H, G = 512, 1024, 512, 512, 512, 1024


def setup_inputs():
    n = np.random.standard_normal
    s = mx_kscale(K)[:, None]
    u = mx_kscale(H)
    packed_xT = pack_weight(n((K, T)) * s)
    packed_pT = pack_weight(n((H, G)) / np.sqrt(4 * H) / u[:, None])
    packed_qT = pack_weight(n((H, G)) / np.sqrt(4 * H) / u[:, None])
    return {
        "x_words": packed_xT[0],
        "x_scales": packed_xT[1],
        "w1": (n((K, H)) / np.sqrt(K) / s * u).astype(np.float32),
        "w2": (n((K, H)) / np.sqrt(K) / s * u).astype(np.float32),
        "rr": (n((H, S))).astype(np.float32),
        "ri": (n((H, S))).astype(np.float32),
        "p_words": packed_pT[0],
        "p_scales": packed_pT[1],
        "q_words": packed_qT[0],
        "q_scales": packed_qT[1],
        "offs": striped(np.random.permutation(T)[:S]),
        "tail": striped(np.random.permutation(G)[:V]),
    }


def reference(x_words, x_scales, w1, w2, rr, ri, p_words, p_scales, q_words, q_scales, offs, tail):
    xq = unpack_weight(x_words, x_scales)[:, unstriped(offs)]
    y = mxq(f64(w1), 0, "e4m3").T @ xq
    e = mxq(f64(w2), 0, "e4m3").T @ xq
    z = y * f64(rr) - (e * f64(ri))
    p_tail = unpack_weight(p_words, p_scales)[:, unstriped(tail)]
    g = y * f64(ri) + e * f64(rr)
    q_tail = unpack_weight(q_words, q_scales)[:, unstriped(tail)]
    s = mxq(z, 0, "e4m3").T @ p_tail + mxq(g, 0, "e4m3").T @ q_tail
    e = np.exp(s - s.max(axis=1, keepdims=True))
    return e / e.sum(axis=1, keepdims=True)

@@ -1,0 +1,183 @@
+from contextlib import ExitStack
+
+import concourse.mybir as mybir
+
+F32 = mybir.dt.float32
+BF16 = mybir.dt.bfloat16
+I32 = mybir.dt.int32
+U32 = mybir.dt.uint32
+U16 = mybir.dt.uint16
+U8 = mybir.dt.uint8
+FP8X4 = mybir.dt.float8_e4m3fn_x4
+ALU = mybir.AluOpType
+ACT = mybir.ActivationFunctionType
+
+P = 128
+PACK = 4
+K = 512
+TABLE = 1024
+PICKED = 512
+BLOCKS = PICKED // P
+HALF = 256
+FLOPS = 4 * 2 * 512 * 512 * 512
+
+
+def tile_picked_zcplx_soft_p_kernel(tc, x_words, x_scales, w1, w2, rr, ri, p_words, p_scales, q_words, q_scales, offs, tail, out):
+    nc = tc.nc
+    with ExitStack() as ctx:
+        keep = ctx.enter_context(tc.tile_pool(name="keep", bufs=1))
+        ring = ctx.enter_context(tc.tile_pool(name="ring", bufs=3))
+        heads = ctx.enter_context(tc.psum_pool(name="heads", bufs=3))
+        scores = ctx.enter_context(tc.psum_pool(name="scores", bufs=2))
+
+        offs_t = keep.tile([P, PICKED // 16], U16, name="offs_t")
+        tail_t = keep.tile([P, PICKED // 16], U16, name="tail_t")
+
+        def scale_window(name):
+            t = keep.tile([P, TABLE], U8, name=name, align_bytes=64)
+            nc.vector.memset(t[:].bitcast(I32), 0)
+            return t
+
+        def load_scales(t, src, queue):
+            for quad in range(4):
+                queue.dma_start(out=t[32 * quad : 32 * quad + 4, :].bitcast(I32), in_=src[0, 4 * quad : 4 * quad + 4, :].bitcast(I32))
+
+        def load_words(name, src):
+            t = keep.tile([P, TABLE], I32, name=name, align_bytes=64)
+            nc.sync.dma_start(out=t[:], in_=src[0].rearrange("p n t -> p (n t)").bitcast(I32))
+            return t
+
+        def load_weight_half(name, w, h):
+            t = keep.tile([P, PACK, HALF], F32, name=name)
+            nc.sync.dma_start(out=t[:], in_=w.rearrange("(p j) c -> p j c", j=PACK)[:, :, h * HALF : (h + 1) * HALF])
+            return t
+
+        def load_relation(c0, width):
+            t = keep.tile([P, 2, PACK, width], F32, name=f"rel{c0}")
+            for part, src in enumerate((rr, ri)):
+                nc.sync.dma_start(out=t[:, part], in_=src.rearrange("(p j) c -> p j c", j=PACK)[:, :, c0 : c0 + width])
+            return [t[:, :, :, c : c + P] for c in range(0, width, P)]
+
+        def gather_words(name, window, offsets):
+            t = keep.tile([P, PICKED], U32, name=name, align_bytes=64)
+            nc.vector.tensor_copy(t[:], window[:].bitcast(U32).indirect(offsets[:]))
+            return t
+
+        def gather_scales(name, window, offsets):
+            t = keep.tile([P, PICKED], U8, name=name, align_bytes=64)
+            nc.vector.tensor_copy(t[:], window[:].indirect(offsets[:]))
+            return t
+
+        def group_weight(name, halves):
+            t = keep.tile([P, PACK * K], BF16, name=name, align_bytes=64)
+            view = t[:].rearrange("p (t m j) -> p m j t", t=PACK, j=PACK)
+            for h, raw in enumerate(halves):
+                nc.scalar.copy(out=view[:, 64 * h : 64 * (h + 1)], in_=raw[:].rearrange("p j (m t) -> p m j t", t=PACK))
+            return t
+
+        def quantize_weight(name, grouped):
+            codes = keep.tile([P, K], U32, name=name + "_codes", align_bytes=64)
+            scales = keep.tile([P, K], U8, name=name + "_scales", align_bytes=64)
+            nc.vector.quantize_mx(out=codes[:].bitcast(FP8X4), scales=scales[:], in_=grouped[:])
+            return codes, scales
+
+        xs_win = scale_window("xs_win")
+        ps_win = scale_window("ps_win")
+        qs_win = scale_window("qs_win")
+        nc.sync.dma_start(offs_t[:], offs)
+        xw_win = load_words("xw_win", x_words)
+        load_scales(xs_win, x_scales, nc.scalar)
+        nc.sync.dma_start(tail_t[:], tail)
+        pw_win = load_words("pw_win", p_words)
+        w1_raw = [load_weight_half(f"w1_raw{h}", w1, h) for h in range(2)]
+        load_scales(ps_win, p_scales, nc.sync)
+        qw_win = load_words("qw_win", q_words)
+        load_scales(qs_win, q_scales, nc.sync)
+        w2_raw = [load_weight_half(f"w2_raw{h}", w2, h) for h in range(2)]
+        rel = load_relation(0, P) + load_relation(P, P) + load_relation(2 * P, 2 * P)
+
+        x_codes = gather_words("x_codes", xw_win, offs_t)
+        x_sc = gather_scales("x_sc", xs_win, offs_t)
+        w1_q = quantize_weight("w1", group_weight("w1_grouped", w1_raw))
+        w2_q = quantize_weight("w2", group_weight("w2_grouped", w2_raw))
+        p_codes = gather_words("p_codes", pw_win, tail_t)
+        p_sc = gather_scales("p_sc", ps_win, tail_t)
+        q_codes = gather_words("q_codes", qw_win, tail_t)
+        q_sc = gather_scales("q_sc", qs_win, tail_t)
+
+        prod, zg, zgq, bank, expd, nmax, total = {}, {}, {}, {}, {}, {}, {}
+
+        def head_products(b, part):
+            codes, scales = (w1_q, w2_q)[part]
+            acc = heads.tile([P, PACK, P], F32, name=f"head{part}")
+            cols = slice(b * P, (b + 1) * P)
+            for j in range(PACK):
+                slot = slice(j * P, (j + 1) * P)
+                nc.tensor.matmul_mx(out=acc[:, j, :], lhsT=codes[:, slot].bitcast(FP8X4), lhsT_scale=scales[:, slot],
+                                    rhs=x_codes[:, cols].bitcast(FP8X4), rhs_scale=x_sc[:, cols], start=True, stop=True)
+            t = ring.tile([P, 2, PACK, P], F32, name=f"prod{part}")
+            nc.vector.tensor_tensor(out=t[:], in0=acc[:].unsqueeze(1).to_broadcast([P, 2, PACK, P]), in1=rel[b], op=ALU.mult)
+            prod[b, part] = t
+
+        def combine(b):
+            t = ring.tile([P, 2, PACK * P], BF16, name="zg", align_bytes=64)
+            walk = "p j (c i) -> p c j i"
+            for which, op in ((0, ALU.subtract), (1, ALU.add)):
+                nc.vector.tensor_tensor(
+                    out=t[:, which, :].rearrange("p (c i j) -> p c j i", i=4, j=PACK),
+                    in0=prod[b, 0][:, which].rearrange(walk, i=4),
+                    in1=prod[b, 1][:, 1 - which].rearrange(walk, i=4), op=op)
+            zg[b] = t
+
+        def score(b):
+            codes = ring.tile([P, 2 * P], U32, name="zg_codes", align_bytes=64)
+            scales = ring.tile([P, 2 * P], U8, name="zg_scales", align_bytes=64)
+            if b < BLOCKS - 1:
+                nc.vector.quantize_mx(out=codes[:].bitcast(FP8X4), scales=scales[:], in_=zg[b][:].rearrange("p a n -> p (a n)"))
+            acc = scores.tile([P, PICKED], F32, name="score")
+            for which, (tc_, ts_) in enumerate(((p_codes, p_sc), (q_codes, q_sc))):
+                cols = slice(which * P, (which + 1) * P)
+                if b == BLOCKS - 1:
+                    nc.vector.quantize_mx(out=codes[:, cols].bitcast(FP8X4), scales=scales[:, cols], in_=zg[b][:, which, :])
+                nc.tensor.matmul_mx(out=acc[:], lhsT=codes[:, cols].bitcast(FP8X4), lhsT_scale=scales[:, cols],
+                                    rhs=tc_[:].bitcast(FP8X4), rhs_scale=ts_[:], start=(which == 0), stop=(which == 1))
+            bank[b] = acc
+
+        def exponentiate(b):
+            m = ring.tile([P, 1], F32, name="nmax")
+            nc.vector.tensor_reduce(out=m[:], in_=bank[b][:], axis=mybir.AxisListType.X, op=ALU.max, negate=True)
+            e = ring.tile([P, PICKED], F32, name="expd")
+            s = ring.tile([P, 1], F32, name="total")
+            nc.scalar.activation(out=e[:], in_=bank[b][:], func=ACT.Exp, bias=m[:], scale=1.0, accum_out=s[:])
+            expd[b], total[b] = e, s
+
+        def normalise(b):
+            r = ring.tile([P, 1], F32, name="recip")
+            nc.vector.reciprocal(out=r[:], in_=total[b][:])
+            rows = slice(b * P, (b + 1) * P)
+            if b < BLOCKS - 1:
+                o = ring.tile([P, PICKED], F32, name="result")
+                nc.scalar.activation(out=o[:], in_=expd[b][:], func=ACT.Copy, scale=r[:])
+                nc.sync.dma_start(out=out[rows, :], in_=o[:])
+            else:
+                o = ring.tile([P, PICKED], F32, name="result")
+                nc.vector.tensor_scalar(out=o[:], in0=expd[b][:], scalar1=r[:], scalar2=None, op0=ALU.mult)
+                nc.sync.dma_start(out=out[rows, :], in_=o[:])
+
+        head_products(0, 0)
+        head_products(1, 0)
+        head_products(0, 1)
+        for b in range(BLOCKS):
+            if 1 <= b < BLOCKS - 1:
+                head_products(b + 1, 0)
+            combine(b)
+            if b >= 2:
+                normalise(b - 2)
+            if b + 1 < BLOCKS:
+                head_products(b + 1, 1)
+            score(b)
+            if b >= 1:
+                exponentiate(b - 1)
+        normalise(BLOCKS - 2)
+        exponentiate(BLOCKS - 1)
+        normalise(BLOCKS - 1)

@@ -27,6 +27,7 @@ def tile_picked_zcplx_soft_p_kernel(tc, x_words, x_scales, w1, w2, rr, ri, p_wor
     with ExitStack() as ctx:
         keep = ctx.enter_context(tc.tile_pool(name="keep", bufs=1))
         ring = ctx.enter_context(tc.tile_pool(name="ring", bufs=3))
+        single = ctx.enter_context(tc.tile_pool(name="single", bufs=1))
         heads = ctx.enter_context(tc.psum_pool(name="heads", bufs=3))
         scores = ctx.enter_context(tc.psum_pool(name="scores", bufs=2))
 
@@ -38,8 +39,8 @@ def tile_picked_zcplx_soft_p_kernel(tc, x_words, x_scales, w1, w2, rr, ri, p_wor
             nc.vector.memset(t[:].bitcast(I32), 0)
             return t
 
-        def load_scales(t, src, queue):
-            for quad in range(4):
+        def load_scales(t, src, queue, quads):
+            for quad in quads:
                 queue.dma_start(out=t[32 * quad : 32 * quad + 4, :].bitcast(I32), in_=src[0, 4 * quad : 4 * quad + 4, :].bitcast(I32))
 
         def load_words(name, src):
@@ -47,9 +48,9 @@ def tile_picked_zcplx_soft_p_kernel(tc, x_words, x_scales, w1, w2, rr, ri, p_wor
             nc.sync.dma_start(out=t[:], in_=src[0].rearrange("p n t -> p (n t)").bitcast(I32))
             return t
 
-        def load_weight_half(name, w, h):
-            t = keep.tile([P, PACK, HALF], F32, name=name)
-            nc.sync.dma_start(out=t[:], in_=w.rearrange("(p j) c -> p j c", j=PACK)[:, :, h * HALF : (h + 1) * HALF])
+        def load_weight(name, w, c0, width):
+            t = keep.tile([P, PACK, width], F32, name=name)
+            nc.sync.dma_start(out=t[:], in_=w.rearrange("(p j) c -> p j c", j=PACK)[:, :, c0 : c0 + width])
             return t
 
         def load_relation(c0, width):
@@ -57,6 +58,11 @@ def tile_picked_zcplx_soft_p_kernel(tc, x_words, x_scales, w1, w2, rr, ri, p_wor
             for part, src in enumerate((rr, ri)):
                 nc.sync.dma_start(out=t[:, part], in_=src.rearrange("(p j) c -> p j c", j=PACK)[:, :, c0 : c0 + width])
             return [t[:, :, :, c : c + P] for c in range(0, width, P)]
+
+        def weave_relation(b, raw):
+            t = keep.tile([P, 2, P * PACK], F32, name=f"woven{b}")
+            nc.scalar.copy(out=t[:].rearrange("p a (c i j) -> p a c j i", i=4, j=PACK), in_=raw.rearrange("p a j (c i) -> p a c j i", i=4))
+            return t
 
         def gather_words(name, window, offsets):
             t = keep.tile([P, PICKED], U32, name=name, align_bytes=64)
@@ -71,8 +77,9 @@ def tile_picked_zcplx_soft_p_kernel(tc, x_words, x_scales, w1, w2, rr, ri, p_wor
         def group_weight(name, halves):
             t = keep.tile([P, PACK * K], BF16, name=name, align_bytes=64)
             view = t[:].rearrange("p (t m j) -> p m j t", t=PACK, j=PACK)
+            span = P // len(halves)
             for h, raw in enumerate(halves):
-                nc.scalar.copy(out=view[:, 64 * h : 64 * (h + 1)], in_=raw[:].rearrange("p j (m t) -> p m j t", t=PACK))
+                nc.scalar.copy(out=view[:, span * h : span * (h + 1)], in_=raw[:].rearrange("p j (m t) -> p m j t", t=PACK))
             return t
 
         def quantize_weight(name, grouped):
@@ -86,20 +93,23 @@ def tile_picked_zcplx_soft_p_kernel(tc, x_words, x_scales, w1, w2, rr, ri, p_wor
         qs_win = scale_window("qs_win")
         nc.sync.dma_start(offs_t[:], offs)
         xw_win = load_words("xw_win", x_words)
-        load_scales(xs_win, x_scales, nc.scalar)
+        load_scales(xs_win, x_scales, nc.scalar, range(4))
         nc.sync.dma_start(tail_t[:], tail)
         pw_win = load_words("pw_win", p_words)
-        w1_raw = [load_weight_half(f"w1_raw{h}", w1, h) for h in range(2)]
-        load_scales(ps_win, p_scales, nc.sync)
+        w1_raw = [load_weight("w1_raw", w1, 0, K)]
+        load_scales(ps_win, p_scales, nc.sync, range(4))
         qw_win = load_words("qw_win", q_words)
-        load_scales(qs_win, q_scales, nc.sync)
-        w2_raw = [load_weight_half(f"w2_raw{h}", w2, h) for h in range(2)]
-        rel = load_relation(0, P) + load_relation(P, P) + load_relation(2 * P, 2 * P)
+        w2_raw = [load_weight("w2_raw0", w2, 0, HALF)]
+        load_scales(qs_win, q_scales, nc.sync, range(2))
+        w2_raw.append(load_weight("w2_raw1", w2, HALF, HALF))
+        load_scales(qs_win, q_scales, nc.sync, range(2, 4))
+        rel_raw = load_relation(0, P) + load_relation(P, P) + load_relation(2 * P, 2 * P)
 
         x_codes = gather_words("x_codes", xw_win, offs_t)
         x_sc = gather_scales("x_sc", xs_win, offs_t)
         w1_q = quantize_weight("w1", group_weight("w1_grouped", w1_raw))
         w2_q = quantize_weight("w2", group_weight("w2_grouped", w2_raw))
+        rel = [weave_relation(b, rel_raw[b]) for b in range(BLOCKS)]
         p_codes = gather_words("p_codes", pw_win, tail_t)
         p_sc = gather_scales("p_sc", ps_win, tail_t)
         q_codes = gather_words("q_codes", qw_win, tail_t)
@@ -115,18 +125,17 @@ def tile_picked_zcplx_soft_p_kernel(tc, x_words, x_scales, w1, w2, rr, ri, p_wor
                 slot = slice(j * P, (j + 1) * P)
                 nc.tensor.matmul_mx(out=acc[:, j, :], lhsT=codes[:, slot].bitcast(FP8X4), lhsT_scale=scales[:, slot],
                                     rhs=x_codes[:, cols].bitcast(FP8X4), rhs_scale=x_sc[:, cols], start=True, stop=True)
-            t = ring.tile([P, 2, PACK, P], F32, name=f"prod{part}")
-            nc.vector.tensor_tensor(out=t[:], in0=acc[:].unsqueeze(1).to_broadcast([P, 2, PACK, P]), in1=rel[b], op=ALU.mult)
+            t = ring.tile([P, 2, P * PACK], F32, name=f"prod{part}")
+            woven = "p a (n j) -> p a n j"
+            nc.vector.tensor_tensor(out=t[:].rearrange(woven, j=PACK), in0=acc[:].rearrange("p j n -> p n j").unsqueeze(1).to_broadcast([P, 2, P, PACK]),
+                                    in1=rel[b][:].rearrange(woven, j=PACK), op=ALU.mult)
             prod[b, part] = t
 
         def combine(b):
-            t = ring.tile([P, 2, PACK * P], BF16, name="zg", align_bytes=64)
-            walk = "p j (c i) -> p c j i"
+            t = single.tile([P, 2, PACK * P], BF16, name="zg", align_bytes=64)
+            engine = nc.gpsimd if b < BLOCKS - 1 else nc.vector
             for which, op in ((0, ALU.subtract), (1, ALU.add)):
-                nc.vector.tensor_tensor(
-                    out=t[:, which, :].rearrange("p (c i j) -> p c j i", i=4, j=PACK),
-                    in0=prod[b, 0][:, which].rearrange(walk, i=4),
-                    in1=prod[b, 1][:, 1 - which].rearrange(walk, i=4), op=op)
+                engine.tensor_tensor(out=t[:, which, :], in0=prod[b, 0][:, which, :], in1=prod[b, 1][:, 1 - which, :], op=op)
             zg[b] = t
 
         def score(b):
@@ -165,19 +174,18 @@ def tile_picked_zcplx_soft_p_kernel(tc, x_words, x_scales, w1, w2, rr, ri, p_wor
                 nc.sync.dma_start(out=out[rows, :], in_=o[:])
 
         head_products(0, 0)
-        head_products(1, 0)
         head_products(0, 1)
         for b in range(BLOCKS):
-            if 1 <= b < BLOCKS - 1:
-                head_products(b + 1, 0)
             combine(b)
+            if b + 1 < BLOCKS:
+                head_products(b + 1, 0)
+                head_products(b + 1, 1)
+            if 1 <= b < BLOCKS - 1:
+                exponentiate(b - 1)
             if b >= 2:
                 normalise(b - 2)
-            if b + 1 < BLOCKS:
-                head_products(b + 1, 1)
             score(b)
-            if b >= 1:
-                exponentiate(b - 1)
-        normalise(BLOCKS - 2)
+        exponentiate(BLOCKS - 2)
         exponentiate(BLOCKS - 1)
+        normalise(BLOCKS - 2)
         normalise(BLOCKS - 1)

@@ -19,6 +19,7 @@ TABLE = 1024
 PICKED = 512
 BLOCKS = PICKED // P
 HALF = 256
+X_ROW, P_ROW, Q_ROW = 4, 8, 12
 FLOPS = 4 * 2 * 512 * 512 * 512
 
 
@@ -28,6 +29,7 @@ def tile_picked_zcplx_soft_p_kernel(tc, x_words, x_scales, w1, w2, rr, ri, p_wor
         keep = ctx.enter_context(tc.tile_pool(name="keep", bufs=1))
         ring = ctx.enter_context(tc.tile_pool(name="ring", bufs=3))
         single = ctx.enter_context(tc.tile_pool(name="single", bufs=1))
+        pairs = ctx.enter_context(tc.tile_pool(name="pairs", bufs=2))
         heads = ctx.enter_context(tc.psum_pool(name="heads", bufs=3))
         scores = ctx.enter_context(tc.psum_pool(name="scores", bufs=2))
 
@@ -39,9 +41,9 @@ def tile_picked_zcplx_soft_p_kernel(tc, x_words, x_scales, w1, w2, rr, ri, p_wor
             nc.vector.memset(t[:].bitcast(I32), 0)
             return t
 
-        def load_scales(t, src, queue, quads):
-            for quad in quads:
-                queue.dma_start(out=t[32 * quad : 32 * quad + 4, :].bitcast(I32), in_=src[0, 4 * quad : 4 * quad + 4, :].bitcast(I32))
+        def load_scales(t, src, first):
+            for quad in range(4):
+                nc.sync.dma_start(out=t[32 * quad + first : 32 * quad + first + 4, :].bitcast(I32), in_=src[0, 4 * quad : 4 * quad + 4, :].bitcast(I32))
 
         def load_words(name, src):
             t = keep.tile([P, TABLE], I32, name=name, align_bytes=64)
@@ -53,15 +55,15 @@ def tile_picked_zcplx_soft_p_kernel(tc, x_words, x_scales, w1, w2, rr, ri, p_wor
             nc.sync.dma_start(out=t[:], in_=w.rearrange("(p j) c -> p j c", j=PACK)[:, :, c0 : c0 + width])
             return t
 
-        def load_relation(c0, width):
-            t = keep.tile([P, 2, PACK, width], F32, name=f"rel{c0}")
-            for part, src in enumerate((rr, ri)):
-                nc.sync.dma_start(out=t[:, part], in_=src.rearrange("(p j) c -> p j c", j=PACK)[:, :, c0 : c0 + width])
-            return [t[:, :, :, c : c + P] for c in range(0, width, P)]
+        def load_relation(part, c0, width):
+            t = keep.tile([P, PACK, width], F32, name=f"rel{part}_{c0}")
+            nc.sync.dma_start(out=t[:], in_=(rr, ri)[part].rearrange("(p j) c -> p j c", j=PACK)[:, :, c0 : c0 + width])
+            return [t[:, :, c : c + P] for c in range(0, width, P)]
 
-        def weave_relation(b, raw):
+        def weave_relation(b):
             t = keep.tile([P, 2, P * PACK], F32, name=f"woven{b}")
-            nc.scalar.copy(out=t[:].rearrange("p a (c i j) -> p a c j i", i=4, j=PACK), in_=raw.rearrange("p a j (c i) -> p a c j i", i=4))
+            for part in range(2):
+                nc.scalar.copy(out=t[:, part, :].rearrange("p (c i j) -> p c j i", i=4, j=PACK), in_=rel_raw[b, part].rearrange("p j (c i) -> p c j i", i=4))
             return t
 
         def gather_words(name, window, offsets):
@@ -93,49 +95,73 @@ def tile_picked_zcplx_soft_p_kernel(tc, x_words, x_scales, w1, w2, rr, ri, p_wor
         qs_win = scale_window("qs_win")
         nc.sync.dma_start(offs_t[:], offs)
         xw_win = load_words("xw_win", x_words)
-        load_scales(xs_win, x_scales, nc.scalar, range(4))
-        nc.sync.dma_start(tail_t[:], tail)
-        pw_win = load_words("pw_win", p_words)
+        load_scales(xs_win, x_scales, X_ROW)
         w1_raw = [load_weight("w1_raw", w1, 0, K)]
-        load_scales(ps_win, p_scales, nc.sync, range(4))
+        nc.sync.dma_start(tail_t[:], tail)
+        load_scales(ps_win, p_scales, P_ROW)
         qw_win = load_words("qw_win", q_words)
-        w2_raw = [load_weight("w2_raw0", w2, 0, HALF)]
-        load_scales(qs_win, q_scales, nc.sync, range(2))
-        w2_raw.append(load_weight("w2_raw1", w2, HALF, HALF))
-        load_scales(qs_win, q_scales, nc.sync, range(2, 4))
-        rel_raw = load_relation(0, P) + load_relation(P, P) + load_relation(2 * P, 2 * P)
+        w2_raw = [load_weight(f"w2_raw{h}", w2, h * HALF, HALF) for h in range(2)]
+        load_scales(qs_win, q_scales, Q_ROW)
+        rel_raw = {(0, 0): load_relation(0, 0, P)[0]}
+        pw_win = load_words("pw_win", p_words)
+        rel_raw[0, 1] = load_relation(1, 0, P)[0]
+        for c0, width in ((P, P), (2 * P, 2 * P)):
+            for part in range(2):
+                for i, piece in enumerate(load_relation(part, c0, width)):
+                    rel_raw[c0 // P + i, part] = piece
 
         x_codes = gather_words("x_codes", xw_win, offs_t)
         x_sc = gather_scales("x_sc", xs_win, offs_t)
         w1_q = quantize_weight("w1", group_weight("w1_grouped", w1_raw))
         w2_q = quantize_weight("w2", group_weight("w2_grouped", w2_raw))
-        rel = [weave_relation(b, rel_raw[b]) for b in range(BLOCKS)]
-        p_codes = gather_words("p_codes", pw_win, tail_t)
+        rel = [weave_relation(b) for b in range(BLOCKS)]
         p_sc = gather_scales("p_sc", ps_win, tail_t)
         q_codes = gather_words("q_codes", qw_win, tail_t)
         q_sc = gather_scales("q_sc", qs_win, tail_t)
+        p_codes = gather_words("p_codes", pw_win, tail_t)
 
         prod, zg, zgq, bank, expd, nmax, total = {}, {}, {}, {}, {}, {}, {}
 
-        def head_products(b, part):
+        def project(b, part):
             codes, scales = (w1_q, w2_q)[part]
             acc = heads.tile([P, PACK, P], F32, name=f"head{part}")
             cols = slice(b * P, (b + 1) * P)
             for j in range(PACK):
                 slot = slice(j * P, (j + 1) * P)
                 nc.tensor.matmul_mx(out=acc[:, j, :], lhsT=codes[:, slot].bitcast(FP8X4), lhsT_scale=scales[:, slot],
-                                    rhs=x_codes[:, cols].bitcast(FP8X4), rhs_scale=x_sc[:, cols], start=True, stop=True)
-            t = ring.tile([P, 2, P * PACK], F32, name=f"prod{part}")
-            woven = "p a (n j) -> p a n j"
-            nc.vector.tensor_tensor(out=t[:].rearrange(woven, j=PACK), in0=acc[:].rearrange("p j n -> p n j").unsqueeze(1).to_broadcast([P, 2, P, PACK]),
-                                    in1=rel[b][:].rearrange(woven, j=PACK), op=ALU.mult)
-            prod[b, part] = t
+                                    rhs=x_codes[:, cols].bitcast(FP8X4), rhs_scale=x_sc[X_ROW:, cols], start=True, stop=True)
+            prod[b, part] = pairs.tile([P, 2, P * PACK], F32, name=f"prod{part}")
+            return acc[:].rearrange("p j n -> p n j")
+
+        def product(b, head, part, which, factor):
+            woven = "p (n j) -> p n j"
+            dst = prod[b, part][:, which, :].rearrange(woven, j=PACK)
+            src = rel[b][:, factor, :].rearrange(woven, j=PACK)
+            if (part, which) == (1, 0):
+                nc.vector.scalar_tensor_tensor(out=dst, in0=head, scalar=-1.0, in1=src, op0=ALU.mult, op1=ALU.mult)
+            else:
+                nc.vector.tensor_tensor(out=dst, in0=head, in1=src, op=ALU.mult)
+
+        def rotate(b):
+            y, e = project(b, 0), project(b, 1)
+            if b == 0:
+                product(b, y, 0, 0, 0)
+                product(b, e, 1, 1, 0)
+                product(b, y, 0, 1, 1)
+            else:
+                woven = "p a (n j) -> p a n j"
+                nc.vector.tensor_tensor(out=prod[b, 0][:].rearrange(woven, j=PACK), in0=y.unsqueeze(1).to_broadcast([P, 2, P, PACK]),
+                                        in1=rel[b][:].rearrange(woven, j=PACK), op=ALU.mult)
+                product(b, e, 1, 1, 0)
+            product(b, e, 1, 0, 1)
 
         def combine(b):
             t = single.tile([P, 2, PACK * P], BF16, name="zg", align_bytes=64)
-            engine = nc.gpsimd if b < BLOCKS - 1 else nc.vector
-            for which, op in ((0, ALU.subtract), (1, ALU.add)):
-                engine.tensor_tensor(out=t[:, which, :], in0=prod[b, 0][:, which, :], in1=prod[b, 1][:, 1 - which, :], op=op)
+            if b < BLOCKS - 1:
+                nc.gpsimd.tensor_tensor(out=t[:], in0=prod[b, 0][:], in1=prod[b, 1][:], op=ALU.add)
+            else:
+                for which in range(2):
+                    nc.vector.tensor_tensor(out=t[:, which, :], in0=prod[b, 0][:, which, :], in1=prod[b, 1][:, which, :], op=ALU.add)
             zg[b] = t
 
         def score(b):
@@ -144,12 +170,12 @@ def tile_picked_zcplx_soft_p_kernel(tc, x_words, x_scales, w1, w2, rr, ri, p_wor
             if b < BLOCKS - 1:
                 nc.vector.quantize_mx(out=codes[:].bitcast(FP8X4), scales=scales[:], in_=zg[b][:].rearrange("p a n -> p (a n)"))
             acc = scores.tile([P, PICKED], F32, name="score")
-            for which, (tc_, ts_) in enumerate(((p_codes, p_sc), (q_codes, q_sc))):
+            for which, (tail_codes, tail_scales) in enumerate(((p_codes[:], p_sc[P_ROW:, :]), (q_codes[:], q_sc[Q_ROW:, :]))):
                 cols = slice(which * P, (which + 1) * P)
                 if b == BLOCKS - 1:
                     nc.vector.quantize_mx(out=codes[:, cols].bitcast(FP8X4), scales=scales[:, cols], in_=zg[b][:, which, :])
                 nc.tensor.matmul_mx(out=acc[:], lhsT=codes[:, cols].bitcast(FP8X4), lhsT_scale=scales[:, cols],
-                                    rhs=tc_[:].bitcast(FP8X4), rhs_scale=ts_[:], start=(which == 0), stop=(which == 1))
+                                    rhs=tail_codes.bitcast(FP8X4), rhs_scale=tail_scales, start=(which == 0), stop=(which == 1))
             bank[b] = acc
 
         def exponentiate(b):
@@ -164,22 +190,24 @@ def tile_picked_zcplx_soft_p_kernel(tc, x_words, x_scales, w1, w2, rr, ri, p_wor
             r = ring.tile([P, 1], F32, name="recip")
             nc.vector.reciprocal(out=r[:], in_=total[b][:])
             rows = slice(b * P, (b + 1) * P)
-            if b < BLOCKS - 1:
-                o = ring.tile([P, PICKED], F32, name="result")
+            o = ring.tile([P, PICKED], F32, name="result")
+            if b < BLOCKS - 2:
                 nc.scalar.activation(out=o[:], in_=expd[b][:], func=ACT.Copy, scale=r[:])
                 nc.sync.dma_start(out=out[rows, :], in_=o[:])
-            else:
-                o = ring.tile([P, PICKED], F32, name="result")
+            elif b == BLOCKS - 2:
                 nc.vector.tensor_scalar(out=o[:], in0=expd[b][:], scalar1=r[:], scalar2=None, op0=ALU.mult)
                 nc.sync.dma_start(out=out[rows, :], in_=o[:])
+            else:
+                for h, queue in enumerate((nc.sync, nc.scalar)):
+                    cols = slice(h * HALF, (h + 1) * HALF)
+                    nc.vector.tensor_scalar(out=o[:, cols], in0=expd[b][:, cols], scalar1=r[:], scalar2=None, op0=ALU.mult)
+                    queue.dma_start(out=out[rows, cols], in_=o[:, cols])
 
-        head_products(0, 0)
-        head_products(0, 1)
+        rotate(0)
         for b in range(BLOCKS):
             combine(b)
             if b + 1 < BLOCKS:
-                head_products(b + 1, 0)
-                head_products(b + 1, 1)
+                rotate(b + 1)
             if 1 <= b < BLOCKS - 1:
                 exponentiate(b - 1)
             if b >= 2:

@@ -120,7 +120,7 @@ def tile_picked_zcplx_soft_p_kernel(tc, x_words, x_scales, w1, w2, rr, ri, p_wor
         q_sc = gather_scales("q_sc", qs_win, tail_t)
         p_codes = gather_words("p_codes", pw_win, tail_t)
 
-        prod, zg, zgq, bank, expd, nmax, total = {}, {}, {}, {}, {}, {}, {}
+        prod, zg, head_bank, bank, expd, total = {}, {}, {}, {}, {}, {}
 
         def project(b, part):
             codes, scales = (w1_q, w2_q)[part]
@@ -130,6 +130,7 @@ def tile_picked_zcplx_soft_p_kernel(tc, x_words, x_scales, w1, w2, rr, ri, p_wor
                 slot = slice(j * P, (j + 1) * P)
                 nc.tensor.matmul_mx(out=acc[:, j, :], lhsT=codes[:, slot].bitcast(FP8X4), lhsT_scale=scales[:, slot],
                                     rhs=x_codes[:, cols].bitcast(FP8X4), rhs_scale=x_sc[X_ROW:, cols], start=True, stop=True)
+            head_bank[part] = acc
             prod[b, part] = pairs.tile([P, 2, P * PACK], F32, name=f"prod{part}")
             return acc[:].rearrange("p j n -> p n j")
 
@@ -154,6 +155,13 @@ def tile_picked_zcplx_soft_p_kernel(tc, x_words, x_scales, w1, w2, rr, ri, p_wor
                                         in1=rel[b][:].rearrange(woven, j=PACK), op=ALU.mult)
                 product(b, e, 1, 1, 0)
             product(b, e, 1, 0, 1)
+
+        def keep_clock(part):
+            codes, scales = (w1_q, w2_q)[part]
+            for j in range(2):
+                slot = slice(j * P, (j + 1) * P)
+                nc.tensor.matmul_mx(out=head_bank[part][:].rearrange("p j n -> p (j n)"), lhsT=codes[:, slot].bitcast(FP8X4), lhsT_scale=scales[:, slot],
+                                    rhs=x_codes[:].bitcast(FP8X4), rhs_scale=x_sc[X_ROW:, :], start=True, stop=True)
 
         def combine(b):
             t = single.tile([P, 2, PACK * P], BF16, name="zg", align_bytes=64)
@@ -208,6 +216,9 @@ def tile_picked_zcplx_soft_p_kernel(tc, x_words, x_scales, w1, w2, rr, ri, p_wor
             combine(b)
             if b + 1 < BLOCKS:
                 rotate(b + 1)
+            if b + 1 == BLOCKS - 1:
+                keep_clock(0)
+                keep_clock(1)
             if 1 <= b < BLOCKS - 1:
                 exponentiate(b - 1)
             if b >= 2:

@@ -42,8 +42,8 @@ def tile_picked_zcplx_soft_p_kernel(tc, x_words, x_scales, w1, w2, rr, ri, p_wor
             return t
 
         def load_scales(t, src, first):
-            for quad in range(4):
-                nc.sync.dma_start(out=t[32 * quad + first : 32 * quad + first + 4, :].bitcast(I32), in_=src[0, 4 * quad : 4 * quad + 4, :].bitcast(I32))
+            for r in range(4):
+                nc.sync.dma_start(out=t[first + r : P : 32, :].bitcast(I32), in_=src[0, r:16:4, :].bitcast(I32))
 
         def load_words(name, src):
             t = keep.tile([P, TABLE], I32, name=name, align_bytes=64)
@@ -96,31 +96,31 @@ def tile_picked_zcplx_soft_p_kernel(tc, x_words, x_scales, w1, w2, rr, ri, p_wor
         nc.sync.dma_start(offs_t[:], offs)
         xw_win = load_words("xw_win", x_words)
         load_scales(xs_win, x_scales, X_ROW)
-        w1_raw = [load_weight("w1_raw", w1, 0, K)]
+        w1_raw = [load_weight(f"w1_raw{h}", w1, h * HALF, HALF) for h in range(2)]
         nc.sync.dma_start(tail_t[:], tail)
         load_scales(ps_win, p_scales, P_ROW)
-        qw_win = load_words("qw_win", q_words)
-        w2_raw = [load_weight(f"w2_raw{h}", w2, h * HALF, HALF) for h in range(2)]
-        load_scales(qs_win, q_scales, Q_ROW)
-        rel_raw = {(0, 0): load_relation(0, 0, P)[0]}
         pw_win = load_words("pw_win", p_words)
-        rel_raw[0, 1] = load_relation(1, 0, P)[0]
-        for c0, width in ((P, P), (2 * P, 2 * P)):
+        w2_raw = [load_weight("w2_raw0", w2, 0, HALF)]
+        qw_win = load_words("qw_win", q_words)
+        load_scales(qs_win, q_scales, Q_ROW)
+        w2_raw.append(load_weight("w2_raw1", w2, HALF, HALF))
+        rel_raw = {}
+        for c0, width in ((0, P), (P, P), (2 * P, 2 * P)):
             for part in range(2):
                 for i, piece in enumerate(load_relation(part, c0, width)):
                     rel_raw[c0 // P + i, part] = piece
 
         x_codes = gather_words("x_codes", xw_win, offs_t)
         x_sc = gather_scales("x_sc", xs_win, offs_t)
-        w1_q = quantize_weight("w1", group_weight("w1_grouped", w1_raw))
-        w2_q = quantize_weight("w2", group_weight("w2_grouped", w2_raw))
-        rel = [weave_relation(b) for b in range(BLOCKS)]
         p_sc = gather_scales("p_sc", ps_win, tail_t)
+        p_codes = gather_words("p_codes", pw_win, tail_t)
+        w1_q = quantize_weight("w1", group_weight("w1_grouped", w1_raw))
         q_codes = gather_words("q_codes", qw_win, tail_t)
         q_sc = gather_scales("q_sc", qs_win, tail_t)
-        p_codes = gather_words("p_codes", pw_win, tail_t)
+        w2_q = quantize_weight("w2", group_weight("w2_grouped", w2_raw))
+        rel = [weave_relation(b) for b in range(BLOCKS)]
 
-        prod, zg, head_bank, bank, expd, total = {}, {}, {}, {}, {}, {}
+        prod, zg, bank, expd, total = {}, {}, {}, {}, {}
 
         def project(b, part):
             codes, scales = (w1_q, w2_q)[part]
@@ -130,7 +130,6 @@ def tile_picked_zcplx_soft_p_kernel(tc, x_words, x_scales, w1, w2, rr, ri, p_wor
                 slot = slice(j * P, (j + 1) * P)
                 nc.tensor.matmul_mx(out=acc[:, j, :], lhsT=codes[:, slot].bitcast(FP8X4), lhsT_scale=scales[:, slot],
                                     rhs=x_codes[:, cols].bitcast(FP8X4), rhs_scale=x_sc[X_ROW:, cols], start=True, stop=True)
-            head_bank[part] = acc
             prod[b, part] = pairs.tile([P, 2, P * PACK], F32, name=f"prod{part}")
             return acc[:].rearrange("p j n -> p n j")
 
@@ -155,13 +154,6 @@ def tile_picked_zcplx_soft_p_kernel(tc, x_words, x_scales, w1, w2, rr, ri, p_wor
                                         in1=rel[b][:].rearrange(woven, j=PACK), op=ALU.mult)
                 product(b, e, 1, 1, 0)
             product(b, e, 1, 0, 1)
-
-        def keep_clock(part):
-            codes, scales = (w1_q, w2_q)[part]
-            for j in range(2):
-                slot = slice(j * P, (j + 1) * P)
-                nc.tensor.matmul_mx(out=head_bank[part][:].rearrange("p j n -> p (j n)"), lhsT=codes[:, slot].bitcast(FP8X4), lhsT_scale=scales[:, slot],
-                                    rhs=x_codes[:].bitcast(FP8X4), rhs_scale=x_sc[X_ROW:, :], start=True, stop=True)
 
         def combine(b):
             t = single.tile([P, 2, PACK * P], BF16, name="zg", align_bytes=64)
@@ -216,9 +208,6 @@ def tile_picked_zcplx_soft_p_kernel(tc, x_words, x_scales, w1, w2, rr, ri, p_wor
             combine(b)
             if b + 1 < BLOCKS:
                 rotate(b + 1)
-            if b + 1 == BLOCKS - 1:
-                keep_clock(0)
-                keep_clock(1)
             if 1 <= b < BLOCKS - 1:
                 exponentiate(b - 1)
             if b >= 2:

@@ -50,9 +50,9 @@ def tile_picked_zcplx_soft_p_kernel(tc, x_words, x_scales, w1, w2, rr, ri, p_wor
             nc.sync.dma_start(out=t[:], in_=src[0].rearrange("p n t -> p (n t)").bitcast(I32))
             return t
 
-        def load_weight(name, w, c0, width):
-            t = keep.tile([P, PACK, width], F32, name=name)
-            nc.sync.dma_start(out=t[:], in_=w.rearrange("(p j) c -> p j c", j=PACK)[:, :, c0 : c0 + width])
+        def load_weight(name, w):
+            t = keep.tile([P, PACK, K], F32, name=name)
+            nc.sync.dma_start(out=t[:], in_=w.rearrange("(p j) c -> p j c", j=PACK))
             return t
 
         def load_relation(part, c0, width):
@@ -76,18 +76,23 @@ def tile_picked_zcplx_soft_p_kernel(tc, x_words, x_scales, w1, w2, rr, ri, p_wor
             nc.vector.tensor_copy(t[:], window[:].indirect(offsets[:]))
             return t
 
-        def group_weight(name, halves):
-            t = keep.tile([P, PACK * K], BF16, name=name, align_bytes=64)
-            view = t[:].rearrange("p (t m j) -> p m j t", t=PACK, j=PACK)
-            span = P // len(halves)
-            for h, raw in enumerate(halves):
-                nc.scalar.copy(out=view[:, span * h : span * (h + 1)], in_=raw[:].rearrange("p j (m t) -> p m j t", t=PACK))
-            return t
-
-        def quantize_weight(name, grouped):
+        def quantize_weight(name, raw, copies):
             codes = keep.tile([P, K], U32, name=name + "_codes", align_bytes=64)
             scales = keep.tile([P, K], U8, name=name + "_scales", align_bytes=64)
-            nc.vector.quantize_mx(out=codes[:].bitcast(FP8X4), scales=scales[:], in_=grouped[:])
+            slots = PACK // len(copies)
+            grouped = []
+            for h, copy in enumerate(copies):
+                t = keep.tile([P, slots * K], BF16, name=f"{name}_grouped{h}", align_bytes=64)
+                copy(out=t[:].rearrange("p (t m j) -> p m j t", t=slots, j=PACK),
+                     in_=raw[:].rearrange("p j (m t) -> p m j t", t=PACK)[:, :, :, h * slots : (h + 1) * slots])
+                grouped.append(t)
+            return codes, scales, grouped
+
+        def quantize(codes, scales, grouped):
+            width = K // len(grouped)
+            for h, t in enumerate(grouped):
+                cols = slice(h * width, (h + 1) * width)
+                nc.vector.quantize_mx(out=codes[:, cols].bitcast(FP8X4), scales=scales[:, cols], in_=t[:])
             return codes, scales
 
         xs_win = scale_window("xs_win")
@@ -95,15 +100,14 @@ def tile_picked_zcplx_soft_p_kernel(tc, x_words, x_scales, w1, w2, rr, ri, p_wor
         qs_win = scale_window("qs_win")
         nc.sync.dma_start(offs_t[:], offs)
         xw_win = load_words("xw_win", x_words)
-        load_scales(xs_win, x_scales, X_ROW)
-        w1_raw = [load_weight(f"w1_raw{h}", w1, h * HALF, HALF) for h in range(2)]
         nc.sync.dma_start(tail_t[:], tail)
-        load_scales(ps_win, p_scales, P_ROW)
         pw_win = load_words("pw_win", p_words)
-        w2_raw = [load_weight("w2_raw0", w2, 0, HALF)]
+        load_scales(xs_win, x_scales, X_ROW)
+        w1_raw = load_weight("w1_raw", w1)
+        load_scales(ps_win, p_scales, P_ROW)
         qw_win = load_words("qw_win", q_words)
+        w2_raw = load_weight("w2_raw", w2)
         load_scales(qs_win, q_scales, Q_ROW)
-        w2_raw.append(load_weight("w2_raw1", w2, HALF, HALF))
         rel_raw = {}
         for c0, width in ((0, P), (P, P), (2 * P, 2 * P)):
             for part in range(2):
@@ -111,13 +115,14 @@ def tile_picked_zcplx_soft_p_kernel(tc, x_words, x_scales, w1, w2, rr, ri, p_wor
                     rel_raw[c0 // P + i, part] = piece
 
         x_codes = gather_words("x_codes", xw_win, offs_t)
+        p_codes = gather_words("p_codes", pw_win, tail_t)
         x_sc = gather_scales("x_sc", xs_win, offs_t)
         p_sc = gather_scales("p_sc", ps_win, tail_t)
-        p_codes = gather_words("p_codes", pw_win, tail_t)
-        w1_q = quantize_weight("w1", group_weight("w1_grouped", w1_raw))
         q_codes = gather_words("q_codes", qw_win, tail_t)
+        w1_q = quantize(*quantize_weight("w1", w1_raw, [nc.scalar.copy]))
+        w2_parts = quantize_weight("w2", w2_raw, [nc.scalar.copy, nc.vector.tensor_copy])
         q_sc = gather_scales("q_sc", qs_win, tail_t)
-        w2_q = quantize_weight("w2", group_weight("w2_grouped", w2_raw))
+        w2_q = quantize(*w2_parts)
         rel = [weave_relation(b) for b in range(BLOCKS)]
 
         prod, zg, bank, expd, total = {}, {}, {}, {}, {}

@@ -28,10 +28,9 @@ def tile_picked_zcplx_soft_p_kernel(tc, x_words, x_scales, w1, w2, rr, ri, p_wor
     with ExitStack() as ctx:
         keep = ctx.enter_context(tc.tile_pool(name="keep", bufs=1))
         ring = ctx.enter_context(tc.tile_pool(name="ring", bufs=3))
-        single = ctx.enter_context(tc.tile_pool(name="single", bufs=1))
-        pairs = ctx.enter_context(tc.tile_pool(name="pairs", bufs=2))
-        heads = ctx.enter_context(tc.psum_pool(name="heads", bufs=3))
-        scores = ctx.enter_context(tc.psum_pool(name="scores", bufs=2))
+        pairs = ctx.enter_context(tc.tile_pool(name="pairs", bufs=3))
+        heads = ctx.enter_context(tc.psum_pool(name="heads", bufs=2))
+        scores = ctx.enter_context(tc.psum_pool(name="scores", bufs=4))
 
         offs_t = keep.tile([P, PICKED // 16], U16, name="offs_t")
         tail_t = keep.tile([P, PICKED // 16], U16, name="tail_t")
@@ -55,16 +54,8 @@ def tile_picked_zcplx_soft_p_kernel(tc, x_words, x_scales, w1, w2, rr, ri, p_wor
             nc.sync.dma_start(out=t[:], in_=w.rearrange("(p j) c -> p j c", j=PACK))
             return t
 
-        def load_relation(part, c0, width):
-            t = keep.tile([P, PACK, width], F32, name=f"rel{part}_{c0}")
-            nc.sync.dma_start(out=t[:], in_=(rr, ri)[part].rearrange("(p j) c -> p j c", j=PACK)[:, :, c0 : c0 + width])
-            return [t[:, :, c : c + P] for c in range(0, width, P)]
-
-        def weave_relation(b):
-            t = keep.tile([P, 2, P * PACK], F32, name=f"woven{b}")
-            for part in range(2):
-                nc.scalar.copy(out=t[:, part, :].rearrange("p (c i j) -> p c j i", i=4, j=PACK), in_=rel_raw[b, part].rearrange("p j (c i) -> p c j i", i=4))
-            return t
+        def load_relation(t, part, c0):
+            nc.sync.dma_start(out=t[:, part], in_=(rr, ri)[part].rearrange("(p j) c -> p j c", j=PACK)[:, :, c0 : c0 + t.shape[3]])
 
         def gather_words(name, window, offsets):
             t = keep.tile([P, PICKED], U32, name=name, align_bytes=64)
@@ -108,11 +99,13 @@ def tile_picked_zcplx_soft_p_kernel(tc, x_words, x_scales, w1, w2, rr, ri, p_wor
         qw_win = load_words("qw_win", q_words)
         w2_raw = load_weight("w2_raw", w2)
         load_scales(qs_win, q_scales, Q_ROW)
-        rel_raw = {}
-        for c0, width in ((0, P), (P, P), (2 * P, 2 * P)):
+        rel0 = keep.tile([P, 2, PACK, P], F32, name="rel0")
+        rel1 = keep.tile([P, 2, PACK, P], F32, name="rel1")
+        rel23 = keep.tile([P, 2, PACK, 2 * P], F32, name="rel23")
+        for t, c0 in ((rel0, 0), (rel1, P), (rel23, 2 * P)):
             for part in range(2):
-                for i, piece in enumerate(load_relation(part, c0, width)):
-                    rel_raw[c0 // P + i, part] = piece
+                load_relation(t, part, c0)
+        rel = [rel0[:], rel1[:], rel23[:, :, :, :P]]
 
         x_codes = gather_words("x_codes", xw_win, offs_t)
         p_codes = gather_words("p_codes", pw_win, tail_t)
@@ -123,9 +116,14 @@ def tile_picked_zcplx_soft_p_kernel(tc, x_words, x_scales, w1, w2, rr, ri, p_wor
         w2_parts = quantize_weight("w2", w2_raw, [nc.scalar.copy, nc.vector.tensor_copy])
         q_sc = gather_scales("q_sc", qs_win, tail_t)
         w2_q = quantize(*w2_parts)
-        rel = [weave_relation(b) for b in range(BLOCKS)]
+        woven = keep.tile([P, 2, P * PACK], F32, name="woven")
+        for part in range(2):
+            nc.scalar.copy(out=woven[:, part, :].rearrange("p (c i j) -> p c j i", i=4, j=PACK),
+                           in_=rel23[:, part, :, P:].rearrange("p j (c i) -> p c j i", i=4))
+        rel.append(woven[:].rearrange("p a (n j) -> p a n j", j=PACK))
 
-        prod, zg, bank, expd, total = {}, {}, {}, {}, {}
+        prod, sums, zg, bank, expd, total = {}, {}, {}, {}, {}, {}
+        last = BLOCKS - 1
 
         def project(b, part):
             codes, scales = (w1_q, w2_q)[part]
@@ -135,39 +133,31 @@ def tile_picked_zcplx_soft_p_kernel(tc, x_words, x_scales, w1, w2, rr, ri, p_wor
                 slot = slice(j * P, (j + 1) * P)
                 nc.tensor.matmul_mx(out=acc[:, j, :], lhsT=codes[:, slot].bitcast(FP8X4), lhsT_scale=scales[:, slot],
                                     rhs=x_codes[:, cols].bitcast(FP8X4), rhs_scale=x_sc[X_ROW:, cols], start=True, stop=True)
-            prod[b, part] = pairs.tile([P, 2, P * PACK], F32, name=f"prod{part}")
-            return acc[:].rearrange("p j n -> p n j")
-
-        def product(b, head, part, which, factor):
-            woven = "p (n j) -> p n j"
-            dst = prod[b, part][:, which, :].rearrange(woven, j=PACK)
-            src = rel[b][:, factor, :].rearrange(woven, j=PACK)
-            if (part, which) == (1, 0):
-                nc.vector.scalar_tensor_tensor(out=dst, in0=head, scalar=-1.0, in1=src, op0=ALU.mult, op1=ALU.mult)
-            else:
-                nc.vector.tensor_tensor(out=dst, in0=head, in1=src, op=ALU.mult)
+            head = acc[:].rearrange("p j n -> p n j") if b == last else acc[:]
+            prod[b, part] = pairs.tile([P, 2] + list(head.shape[1:]), F32, name=f"prod{part}")
+            return head
 
         def rotate(b):
             y, e = project(b, 0), project(b, 1)
             if b == 0:
-                product(b, y, 0, 0, 0)
-                product(b, e, 1, 1, 0)
-                product(b, y, 0, 1, 1)
+                for a in range(2):
+                    nc.vector.tensor_tensor(out=prod[b, 0][:, a], in0=y, in1=rel[b][:, a], op=ALU.mult)
             else:
-                woven = "p a (n j) -> p a n j"
-                nc.vector.tensor_tensor(out=prod[b, 0][:].rearrange(woven, j=PACK), in0=y.unsqueeze(1).to_broadcast([P, 2, P, PACK]),
-                                        in1=rel[b][:].rearrange(woven, j=PACK), op=ALU.mult)
-                product(b, e, 1, 1, 0)
-            product(b, e, 1, 0, 1)
+                nc.vector.tensor_tensor(out=prod[b, 0][:], in0=y.unsqueeze(1).to_broadcast(list(prod[b, 0].shape)), in1=rel[b], op=ALU.mult)
+            nc.vector.tensor_tensor(out=prod[b, 1][:, 1], in0=e, in1=rel[b][:, 0], op=ALU.mult)
+            nc.vector.scalar_tensor_tensor(out=prod[b, 1][:, 0], in0=e, scalar=-1.0, in1=rel[b][:, 1], op0=ALU.mult, op1=ALU.mult)
 
         def combine(b):
-            t = single.tile([P, 2, PACK * P], BF16, name="zg", align_bytes=64)
-            if b < BLOCKS - 1:
-                nc.gpsimd.tensor_tensor(out=t[:], in0=prod[b, 0][:], in1=prod[b, 1][:], op=ALU.add)
-            else:
-                for which in range(2):
-                    nc.vector.tensor_tensor(out=t[:, which, :], in0=prod[b, 0][:, which, :], in1=prod[b, 1][:, which, :], op=ALU.add)
-            zg[b] = t
+            t = keep.tile([P, 2, PACK, P], F32, name=f"sums{b}", tag=("sums0", "sums1", "zg0")[b], align_bytes=64)
+            nc.gpsimd.tensor_tensor(out=t[:], in0=prod[b, 0][:], in1=prod[b, 1][:], op=ALU.add)
+            sums[b] = t
+
+        def weave(b):
+            zg[b] = keep.tile([P, 2, P * PACK], BF16, name=f"zg{b}", align_bytes=64)
+            nc.scalar.copy(out=zg[b][:].rearrange("p a (c i j) -> p a c j i", i=4, j=PACK), in_=sums[b][:].rearrange("p a j (c i) -> p a c j i", i=4))
+
+        def combine_last(a):
+            nc.vector.tensor_tensor(out=zg[last][:, a].rearrange("p (n j) -> p n j", j=PACK), in0=prod[last, 0][:, a], in1=prod[last, 1][:, a], op=ALU.add)
 
         def score(b):
             codes = ring.tile([P, 2 * P], U32, name="zg_codes", align_bytes=64)
@@ -196,10 +186,10 @@ def tile_picked_zcplx_soft_p_kernel(tc, x_words, x_scales, w1, w2, rr, ri, p_wor
             nc.vector.reciprocal(out=r[:], in_=total[b][:])
             rows = slice(b * P, (b + 1) * P)
             o = ring.tile([P, PICKED], F32, name="result")
-            if b < BLOCKS - 2:
+            if b == 0:
                 nc.scalar.activation(out=o[:], in_=expd[b][:], func=ACT.Copy, scale=r[:])
                 nc.sync.dma_start(out=out[rows, :], in_=o[:])
-            elif b == BLOCKS - 2:
+            elif b < last:
                 nc.vector.tensor_scalar(out=o[:], in0=expd[b][:], scalar1=r[:], scalar2=None, op0=ALU.mult)
                 nc.sync.dma_start(out=out[rows, :], in_=o[:])
             else:
@@ -209,16 +199,25 @@ def tile_picked_zcplx_soft_p_kernel(tc, x_words, x_scales, w1, w2, rr, ri, p_wor
                     queue.dma_start(out=out[rows, cols], in_=o[:, cols])
 
         rotate(0)
-        for b in range(BLOCKS):
-            combine(b)
-            if b + 1 < BLOCKS:
-                rotate(b + 1)
-            if 1 <= b < BLOCKS - 1:
-                exponentiate(b - 1)
-            if b >= 2:
-                normalise(b - 2)
-            score(b)
-        exponentiate(BLOCKS - 2)
-        exponentiate(BLOCKS - 1)
-        normalise(BLOCKS - 2)
-        normalise(BLOCKS - 1)
+        combine(0)
+        rotate(1)
+        weave(0)
+        combine(1)
+        rotate(2)
+        score(0)
+        weave(1)
+        combine(2)
+        rotate(3)
+        exponentiate(0)
+        score(1)
+        weave(2)
+        zg[last] = keep.tile([P, 2, P * PACK], BF16, name="zg_last", align_bytes=64)
+        combine_last(0)
+        normalise(0)
+        score(2)
+        combine_last(1)
+        score(3)
+        for b in range(1, BLOCKS):
+            exponentiate(b)
+        for b in range(1, BLOCKS):
+            normalise(b)

@@ -28,7 +28,6 @@ def tile_picked_zcplx_soft_p_kernel(tc, x_words, x_scales, w1, w2, rr, ri, p_wor
     with ExitStack() as ctx:
         keep = ctx.enter_context(tc.tile_pool(name="keep", bufs=1))
         ring = ctx.enter_context(tc.tile_pool(name="ring", bufs=3))
-        pairs = ctx.enter_context(tc.tile_pool(name="pairs", bufs=3))
         heads = ctx.enter_context(tc.psum_pool(name="heads", bufs=2))
         scores = ctx.enter_context(tc.psum_pool(name="scores", bufs=4))
 
@@ -49,9 +48,9 @@ def tile_picked_zcplx_soft_p_kernel(tc, x_words, x_scales, w1, w2, rr, ri, p_wor
             nc.sync.dma_start(out=t[:], in_=src[0].rearrange("p n t -> p (n t)").bitcast(I32))
             return t
 
-        def load_weight(name, w):
-            t = keep.tile([P, PACK, K], F32, name=name)
-            nc.sync.dma_start(out=t[:], in_=w.rearrange("(p j) c -> p j c", j=PACK))
+        def load_weight(name, w, c0, width):
+            t = keep.tile([P, PACK, width], F32, name=name)
+            nc.sync.dma_start(out=t[:], in_=w.rearrange("(p j) c -> p j c", j=PACK)[:, :, c0 : c0 + width])
             return t
 
         def load_relation(t, part, c0):
@@ -67,19 +66,14 @@ def tile_picked_zcplx_soft_p_kernel(tc, x_words, x_scales, w1, w2, rr, ri, p_wor
             nc.vector.tensor_copy(t[:], window[:].indirect(offsets[:]))
             return t
 
-        def quantize_weight(name, raw, copies):
-            codes = keep.tile([P, K], U32, name=name + "_codes", align_bytes=64)
-            scales = keep.tile([P, K], U8, name=name + "_scales", align_bytes=64)
-            slots = PACK // len(copies)
-            grouped = []
-            for h, copy in enumerate(copies):
-                t = keep.tile([P, slots * K], BF16, name=f"{name}_grouped{h}", align_bytes=64)
-                copy(out=t[:].rearrange("p (t m j) -> p m j t", t=slots, j=PACK),
-                     in_=raw[:].rearrange("p j (m t) -> p m j t", t=PACK)[:, :, :, h * slots : (h + 1) * slots])
-                grouped.append(t)
-            return codes, scales, grouped
+        def group(copy, grouped, raw, piece, pieces, first, count):
+            span = P // pieces
+            copy(out=grouped[:].rearrange("p (t m j) -> p m j t", t=count, j=PACK)[:, span * piece : span * (piece + 1)],
+                 in_=raw[:].rearrange("p j (m t) -> p m j t", t=PACK)[:, :, :, first : first + count])
 
-        def quantize(codes, scales, grouped):
+        def quantize_weight(name, grouped, tag):
+            codes = keep.tile([P, K], U32, name=name + "_codes", tag=tag, align_bytes=64)
+            scales = keep.tile([P, K], U8, name=name + "_scales", align_bytes=64)
             width = K // len(grouped)
             for h, t in enumerate(grouped):
                 cols = slice(h * width, (h + 1) * width)
@@ -94,11 +88,12 @@ def tile_picked_zcplx_soft_p_kernel(tc, x_words, x_scales, w1, w2, rr, ri, p_wor
         nc.sync.dma_start(tail_t[:], tail)
         pw_win = load_words("pw_win", p_words)
         load_scales(xs_win, x_scales, X_ROW)
-        w1_raw = load_weight("w1_raw", w1)
+        w1_raw = load_weight("w1_raw", w1, 0, K)
         load_scales(ps_win, p_scales, P_ROW)
         qw_win = load_words("qw_win", q_words)
-        w2_raw = load_weight("w2_raw", w2)
+        w2_raw = [load_weight("w2_raw0", w2, 0, HALF)]
         load_scales(qs_win, q_scales, Q_ROW)
+        w2_raw.append(load_weight("w2_raw1", w2, HALF, HALF))
         rel0 = keep.tile([P, 2, PACK, P], F32, name="rel0")
         rel1 = keep.tile([P, 2, PACK, P], F32, name="rel1")
         rel23 = keep.tile([P, 2, PACK, 2 * P], F32, name="rel23")
@@ -112,10 +107,16 @@ def tile_picked_zcplx_soft_p_kernel(tc, x_words, x_scales, w1, w2, rr, ri, p_wor
         x_sc = gather_scales("x_sc", xs_win, offs_t)
         p_sc = gather_scales("p_sc", ps_win, tail_t)
         q_codes = gather_words("q_codes", qw_win, tail_t)
-        w1_q = quantize(*quantize_weight("w1", w1_raw, [nc.scalar.copy]))
-        w2_parts = quantize_weight("w2", w2_raw, [nc.scalar.copy, nc.vector.tensor_copy])
         q_sc = gather_scales("q_sc", qs_win, tail_t)
-        w2_q = quantize(*w2_parts)
+        w1_grouped = keep.tile([P, PACK * K], BF16, name="w1_grouped", align_bytes=64)
+        group(nc.scalar.copy, w1_grouped, w1_raw, 0, 1, 0, PACK)
+        w1_q = quantize_weight("w1", [w1_grouped], "qs_win")
+        w2_grouped = [keep.tile([P, 2 * K], BF16, name=f"w2_grouped{h}", align_bytes=64) for h in range(2)]
+        group(nc.scalar.copy, w2_grouped[1], w2_raw[0], 0, 2, 2, 2)
+        group(nc.scalar.copy, w2_grouped[0], w2_raw[0], 0, 2, 0, 2)
+        group(nc.scalar.copy, w2_grouped[0], w2_raw[1], 1, 2, 0, 2)
+        group(nc.vector.tensor_copy, w2_grouped[1], w2_raw[1], 1, 2, 2, 2)
+        w2_q = quantize_weight("w2", w2_grouped, "w2_codes")
         woven = keep.tile([P, 2, P * PACK], F32, name="woven")
         for part in range(2):
             nc.scalar.copy(out=woven[:, part, :].rearrange("p (c i j) -> p c j i", i=4, j=PACK),
@@ -134,7 +135,7 @@ def tile_picked_zcplx_soft_p_kernel(tc, x_words, x_scales, w1, w2, rr, ri, p_wor
                 nc.tensor.matmul_mx(out=acc[:, j, :], lhsT=codes[:, slot].bitcast(FP8X4), lhsT_scale=scales[:, slot],
                                     rhs=x_codes[:, cols].bitcast(FP8X4), rhs_scale=x_sc[X_ROW:, cols], start=True, stop=True)
             head = acc[:].rearrange("p j n -> p n j") if b == last else acc[:]
-            prod[b, part] = pairs.tile([P, 2] + list(head.shape[1:]), F32, name=f"prod{part}")
+            prod[b, part] = keep.tile([P, 2] + list(head.shape[1:]), F32, name=f"prod{b}_{part}", tag="w2_grouped1" if (b, part) == (0, 0) else f"prod{b}_{part}", align_bytes=64)
             return head
 
         def rotate(b):
@@ -149,7 +150,11 @@ def tile_picked_zcplx_soft_p_kernel(tc, x_words, x_scales, w1, w2, rr, ri, p_wor
 
         def combine(b):
             t = keep.tile([P, 2, PACK, P], F32, name=f"sums{b}", tag=("sums0", "sums1", "zg0")[b], align_bytes=64)
-            nc.gpsimd.tensor_tensor(out=t[:], in0=prod[b, 0][:], in1=prod[b, 1][:], op=ALU.add)
+            if b == 0:
+                for a in (1, 0):
+                    nc.gpsimd.tensor_tensor(out=t[:, a], in0=prod[b, 0][:, a], in1=prod[b, 1][:, a], op=ALU.add)
+            else:
+                nc.gpsimd.tensor_tensor(out=t[:], in0=prod[b, 0][:], in1=prod[b, 1][:], op=ALU.add)
             sums[b] = t
 
         def weave(b):
@@ -174,10 +179,10 @@ def tile_picked_zcplx_soft_p_kernel(tc, x_words, x_scales, w1, w2, rr, ri, p_wor
             bank[b] = acc
 
         def exponentiate(b):
-            m = ring.tile([P, 1], F32, name="nmax")
+            m = keep.tile([P, 1], F32, name=f"nmax{b}", tag="total1" if b == last else f"nmax{b}")
             nc.vector.tensor_reduce(out=m[:], in_=bank[b][:], axis=mybir.AxisListType.X, op=ALU.max, negate=True)
             e = ring.tile([P, PICKED], F32, name="expd")
-            s = ring.tile([P, 1], F32, name="total")
+            s = keep.tile([P, 1], F32, name=f"total{b}")
             nc.scalar.activation(out=e[:], in_=bank[b][:], func=ACT.Exp, bias=m[:], scale=1.0, accum_out=s[:])
             expd[b], total[b] = e, s
 
@@ -188,6 +193,9 @@ def tile_picked_zcplx_soft_p_kernel(tc, x_words, x_scales, w1, w2, rr, ri, p_wor
             o = ring.tile([P, PICKED], F32, name="result")
             if b == 0:
                 nc.scalar.activation(out=o[:], in_=expd[b][:], func=ACT.Copy, scale=r[:])
+                nc.sync.dma_start(out=out[rows, :], in_=o[:])
+            elif b == 1:
+                nc.gpsimd.tensor_scalar(out=o[:], in0=expd[b][:], scalar1=r[:], scalar2=0.0, op0=ALU.mult, op1=ALU.add)
                 nc.sync.dma_start(out=out[rows, :], in_=o[:])
             elif b < last:
                 nc.vector.tensor_scalar(out=o[:], in0=expd[b][:], scalar1=r[:], scalar2=None, op0=ALU.mult)
@@ -216,8 +224,10 @@ def tile_picked_zcplx_soft_p_kernel(tc, x_words, x_scales, w1, w2, rr, ri, p_wor
         normalise(0)
         score(2)
         combine_last(1)
+        exponentiate(1)
         score(3)
-        for b in range(1, BLOCKS):
-            exponentiate(b)
-        for b in range(1, BLOCKS):
-            normalise(b)
+        exponentiate(2)
+        normalise(1)
+        exponentiate(3)
+        normalise(2)
+        normalise(3)

@@ -75,9 +75,9 @@ def tile_picked_zcplx_soft_p_kernel(tc, x_words, x_scales, w1, w2, rr, ri, p_wor
             codes = keep.tile([P, K], U32, name=name + "_codes", tag=tag, align_bytes=64)
             scales = keep.tile([P, K], U8, name=name + "_scales", align_bytes=64)
             width = K // len(grouped)
-            for h, t in enumerate(grouped):
+            for h in reversed(range(len(grouped))):
                 cols = slice(h * width, (h + 1) * width)
-                nc.vector.quantize_mx(out=codes[:, cols].bitcast(FP8X4), scales=scales[:, cols], in_=t[:])
+                nc.vector.quantize_mx(out=codes[:, cols].bitcast(FP8X4), scales=scales[:, cols], in_=grouped[h][:])
             return codes, scales
 
         xs_win = scale_window("xs_win")
@@ -85,11 +85,11 @@ def tile_picked_zcplx_soft_p_kernel(tc, x_words, x_scales, w1, w2, rr, ri, p_wor
         qs_win = scale_window("qs_win")
         nc.sync.dma_start(offs_t[:], offs)
         xw_win = load_words("xw_win", x_words)
-        nc.sync.dma_start(tail_t[:], tail)
-        pw_win = load_words("pw_win", p_words)
         load_scales(xs_win, x_scales, X_ROW)
         w1_raw = load_weight("w1_raw", w1, 0, K)
+        nc.sync.dma_start(tail_t[:], tail)
         load_scales(ps_win, p_scales, P_ROW)
+        pw_win = load_words("pw_win", p_words)
         qw_win = load_words("qw_win", q_words)
         w2_raw = [load_weight("w2_raw0", w2, 0, HALF)]
         load_scales(qs_win, q_scales, Q_ROW)
@@ -103,14 +103,14 @@ def tile_picked_zcplx_soft_p_kernel(tc, x_words, x_scales, w1, w2, rr, ri, p_wor
         rel = [rel0[:], rel1[:], rel23[:, :, :, :P]]
 
         x_codes = gather_words("x_codes", xw_win, offs_t)
-        p_codes = gather_words("p_codes", pw_win, tail_t)
         x_sc = gather_scales("x_sc", xs_win, offs_t)
         p_sc = gather_scales("p_sc", ps_win, tail_t)
+        p_codes = gather_words("p_codes", pw_win, tail_t)
         q_codes = gather_words("q_codes", qw_win, tail_t)
-        q_sc = gather_scales("q_sc", qs_win, tail_t)
         w1_grouped = keep.tile([P, PACK * K], BF16, name="w1_grouped", align_bytes=64)
         group(nc.scalar.copy, w1_grouped, w1_raw, 0, 1, 0, PACK)
-        w1_q = quantize_weight("w1", [w1_grouped], "qs_win")
+        w1_q = quantize_weight("w1", [w1_grouped], "qw_win")
+        q_sc = gather_scales("q_sc", qs_win, tail_t)
         w2_grouped = [keep.tile([P, 2 * K], BF16, name=f"w2_grouped{h}", align_bytes=64) for h in range(2)]
         group(nc.scalar.copy, w2_grouped[1], w2_raw[0], 0, 2, 2, 2)
         group(nc.scalar.copy, w2_grouped[0], w2_raw[0], 0, 2, 0, 2)
@@ -135,7 +135,7 @@ def tile_picked_zcplx_soft_p_kernel(tc, x_words, x_scales, w1, w2, rr, ri, p_wor
                 nc.tensor.matmul_mx(out=acc[:, j, :], lhsT=codes[:, slot].bitcast(FP8X4), lhsT_scale=scales[:, slot],
                                     rhs=x_codes[:, cols].bitcast(FP8X4), rhs_scale=x_sc[X_ROW:, cols], start=True, stop=True)
             head = acc[:].rearrange("p j n -> p n j") if b == last else acc[:]
-            prod[b, part] = keep.tile([P, 2] + list(head.shape[1:]), F32, name=f"prod{b}_{part}", tag="w2_grouped1" if (b, part) == (0, 0) else f"prod{b}_{part}", align_bytes=64)
+            prod[b, part] = keep.tile([P, 2] + list(head.shape[1:]), F32, name=f"prod{b}_{part}", tag="w2_grouped0" if (b, part) == (0, 0) else f"prod{b}_{part}", align_bytes=64)
             return head
 
         def rotate(b):

@@ -1,6 +1,7 @@
 from contextlib import ExitStack
 
 import concourse.mybir as mybir
+from concourse.masks import make_identity
 
 F32 = mybir.dt.float32
 BF16 = mybir.dt.bfloat16
@@ -20,6 +21,7 @@ PICKED = 512
 BLOCKS = PICKED // P
 HALF = 256
 X_ROW, P_ROW, Q_ROW = 4, 8, 12
+EARLY = 2
 FLOPS = 4 * 2 * 512 * 512 * 512
 
 
@@ -28,8 +30,8 @@ def tile_picked_zcplx_soft_p_kernel(tc, x_words, x_scales, w1, w2, rr, ri, p_wor
     with ExitStack() as ctx:
         keep = ctx.enter_context(tc.tile_pool(name="keep", bufs=1))
         ring = ctx.enter_context(tc.tile_pool(name="ring", bufs=3))
-        heads = ctx.enter_context(tc.psum_pool(name="heads", bufs=2))
-        scores = ctx.enter_context(tc.psum_pool(name="scores", bufs=4))
+        laid = ctx.enter_context(tc.tile_pool(name="laid", bufs=1))
+        psum = ctx.enter_context(tc.psum_pool(name="psum", bufs=1))
 
         offs_t = keep.tile([P, PICKED // 16], U16, name="offs_t")
         tail_t = keep.tile([P, PICKED // 16], U16, name="tail_t")
@@ -111,12 +113,14 @@ def tile_picked_zcplx_soft_p_kernel(tc, x_words, x_scales, w1, w2, rr, ri, p_wor
         group(nc.scalar.copy, w1_grouped, w1_raw, 0, 1, 0, PACK)
         w1_q = quantize_weight("w1", [w1_grouped], "qw_win")
         q_sc = gather_scales("q_sc", qs_win, tail_t)
-        w2_grouped = [keep.tile([P, 2 * K], BF16, name=f"w2_grouped{h}", align_bytes=64) for h in range(2)]
+        w2_grouped = [laid.tile([P, 2 * K], BF16, name=f"w2_grouped{h}", align_bytes=64, offset=(9216, 12288)[h]) for h in range(2)]
         group(nc.scalar.copy, w2_grouped[1], w2_raw[0], 0, 2, 2, 2)
         group(nc.scalar.copy, w2_grouped[0], w2_raw[0], 0, 2, 0, 2)
         group(nc.scalar.copy, w2_grouped[0], w2_raw[1], 1, 2, 0, 2)
         group(nc.vector.tensor_copy, w2_grouped[1], w2_raw[1], 1, 2, 2, 2)
         w2_q = quantize_weight("w2", w2_grouped, "w2_codes")
+        ident = keep.tile([P, P], F32, name="ident")
+        make_identity(nc, ident[:])
         woven = keep.tile([P, 2, P * PACK], F32, name="woven")
         for part in range(2):
             nc.scalar.copy(out=woven[:, part, :].rearrange("p (c i j) -> p c j i", i=4, j=PACK),
@@ -128,38 +132,80 @@ def tile_picked_zcplx_soft_p_kernel(tc, x_words, x_scales, w1, w2, rr, ri, p_wor
 
         def project(b, part):
             codes, scales = (w1_q, w2_q)[part]
-            acc = heads.tile([P, PACK, P], F32, name=f"head{part}")
+            acc = psum.tile([P, PACK, P], F32, name=f"head{b}_{part}", tag=f"head{part}_{b % 2}")
             cols = slice(b * P, (b + 1) * P)
             for j in range(PACK):
                 slot = slice(j * P, (j + 1) * P)
                 nc.tensor.matmul_mx(out=acc[:, j, :], lhsT=codes[:, slot].bitcast(FP8X4), lhsT_scale=scales[:, slot],
                                     rhs=x_codes[:, cols].bitcast(FP8X4), rhs_scale=x_sc[X_ROW:, cols], start=True, stop=True)
             head = acc[:].rearrange("p j n -> p n j") if b == last else acc[:]
-            prod[b, part] = keep.tile([P, 2] + list(head.shape[1:]), F32, name=f"prod{b}_{part}", tag="w2_grouped0" if (b, part) == (0, 0) else f"prod{b}_{part}", align_bytes=64)
+            if b >= EARLY:
+                prod[b, part] = keep.tile([P, 2] + list(head.shape[1:]), F32, name=f"prod{b}_{part}", align_bytes=64)
             return head
 
         def rotate(b):
             y, e = project(b, 0), project(b, 1)
-            if b == 0:
-                for a in range(2):
-                    nc.vector.tensor_tensor(out=prod[b, 0][:, a], in0=y, in1=rel[b][:, a], op=ALU.mult)
-            else:
+            if True:
                 nc.vector.tensor_tensor(out=prod[b, 0][:], in0=y.unsqueeze(1).to_broadcast(list(prod[b, 0].shape)), in1=rel[b], op=ALU.mult)
             nc.vector.tensor_tensor(out=prod[b, 1][:, 1], in0=e, in1=rel[b][:, 0], op=ALU.mult)
             nc.vector.scalar_tensor_tensor(out=prod[b, 1][:, 0], in0=e, scalar=-1.0, in1=rel[b][:, 1], op0=ALU.mult, op1=ALU.mult)
 
         def combine(b):
-            t = keep.tile([P, 2, PACK, P], F32, name=f"sums{b}", tag=("sums0", "sums1", "zg0")[b], align_bytes=64)
-            if b == 0:
-                for a in (1, 0):
-                    nc.gpsimd.tensor_tensor(out=t[:, a], in0=prod[b, 0][:, a], in1=prod[b, 1][:, a], op=ALU.add)
-            else:
+            t = laid.tile([P, 2, PACK, P], F32, name=f"sums{b}", align_bytes=64, offset=0)
+            if True:
                 nc.gpsimd.tensor_tensor(out=t[:], in0=prod[b, 0][:], in1=prod[b, 1][:], op=ALU.add)
             sums[b] = t
 
         def weave(b):
             zg[b] = keep.tile([P, 2, P * PACK], BF16, name=f"zg{b}", align_bytes=64)
             nc.scalar.copy(out=zg[b][:].rearrange("p a (c i j) -> p a c j i", i=4, j=PACK), in_=sums[b][:].rearrange("p a j (c i) -> p a c j i", i=4))
+
+        heads, y_rr, y_ri, e_r, z_sum, g_turned, g_pairs, g_words = {}, {}, {}, {}, {}, {}, {}, {}
+        y_sb = keep.tile([P, EARLY, PACK, P], F32, name="y_sb", tag="w2_raw1")
+
+        def copy_y(b):
+            nc.scalar.copy(out=y_sb[:, b], in_=heads[b, 0])
+
+        def mul_y_rr(b):
+            y_rr[b] = laid.tile([P, PACK, P], F32, name=f"y_rr{b}", align_bytes=64, offset=(10240, 16384)[b])
+            nc.gpsimd.tensor_tensor(out=y_rr[b][:], in0=y_sb[:, b], in1=rel[b][:, 0], op=ALU.mult)
+
+        def mul_y_ri(b):
+            y_ri[b] = laid.tile([P, PACK, P], F32, name=f"y_ri{b}", align_bytes=64, offset=(8192, 14336)[b])
+            nc.vector.tensor_tensor(out=y_ri[b][:], in0=heads[b, 0], in1=rel[b][:, 1], op=ALU.mult)
+
+        def mul_e(b):
+            e_r[b] = keep.tile([P, 2, PACK, P], F32, name=f"e_r{b}")
+            nc.vector.tensor_tensor(out=e_r[b][:], in0=heads[b, 1].unsqueeze(1).to_broadcast([P, 2, PACK, P]), in1=rel[b], op=ALU.mult)
+
+        def sub_z(b):
+            z_sum[b] = keep.tile([P, PACK, P], F32, name=f"z_sum{b}")
+            nc.gpsimd.tensor_tensor(out=z_sum[b][:], in0=y_rr[b][:], in1=e_r[b][:, 1], op=ALU.subtract)
+
+        def weave_z(b):
+            zg[b] = laid.tile([P, 2, P * PACK], BF16, name=f"zg{b}", align_bytes=64, offset=(2560, 4608)[b])
+            nc.scalar.copy(out=zg[b][:, 0, :].rearrange("p (c i j) -> p c j i", i=4, j=PACK), in_=z_sum[b][:].rearrange("p j (c i) -> p c j i", i=4))
+
+        def add_g(b):
+            acc = psum.tile([P, PACK, P], F32, name=f"g_turned{b}", tag="bank_a")
+            for j in range(PACK):
+                for term, src in enumerate((y_ri[b][:, j, :], e_r[b][:, 0, j, :])):
+                    nc.tensor.matmul(acc[:, j, :], lhsT=src, rhs=ident[:], is_transpose=True, start=(term == 0), stop=(term == 1))
+            g_turned[b] = acc
+
+        def round_g(b):
+            g_pairs[b] = laid.tile([P, PACK * P], BF16, name=f"g_pairs{b}", align_bytes=64, offset=(4096, 6656)[b])
+            nc.scalar.copy(out=g_pairs[b][:].rearrange("t (u p e) -> t u p e", u=2, e=2), in_=g_turned[b][:].rearrange("t (u e) p -> t u p e", e=2))
+
+        def turn_g(b):
+            acc = psum.tile([P, 2, P], F32, name=f"g_words{b}", tag="bank_b")
+            words = g_pairs[b][:].bitcast(F32)
+            for u in range(2):
+                nc.tensor.transpose(acc[:, u, :], words[:, u * P : (u + 1) * P], ident[:])
+            g_words[b] = acc
+
+        def weave_g(b):
+            nc.scalar.copy(out=zg[b][:, 1, :].bitcast(F32).rearrange("p (n u) -> p n u", u=2), in_=g_words[b][:].rearrange("p u n -> p n u"))
 
         def combine_last(a):
             nc.vector.tensor_tensor(out=zg[last][:, a].rearrange("p (n j) -> p n j", j=PACK), in0=prod[last, 0][:, a], in1=prod[last, 1][:, a], op=ALU.add)
@@ -169,7 +215,7 @@ def tile_picked_zcplx_soft_p_kernel(tc, x_words, x_scales, w1, w2, rr, ri, p_wor
             scales = ring.tile([P, 2 * P], U8, name="zg_scales", align_bytes=64)
             if b < BLOCKS - 1:
                 nc.vector.quantize_mx(out=codes[:].bitcast(FP8X4), scales=scales[:], in_=zg[b][:].rearrange("p a n -> p (a n)"))
-            acc = scores.tile([P, PICKED], F32, name="score")
+            acc = psum.tile([P, PICKED], F32, name=f"score{b}", tag=("bank_c", "bank_d", "bank_a", "bank_b")[b])
             for which, (tail_codes, tail_scales) in enumerate(((p_codes[:], p_sc[P_ROW:, :]), (q_codes[:], q_sc[Q_ROW:, :]))):
                 cols = slice(which * P, (which + 1) * P)
                 if b == BLOCKS - 1:
@@ -206,14 +252,31 @@ def tile_picked_zcplx_soft_p_kernel(tc, x_words, x_scales, w1, w2, rr, ri, p_wor
                     nc.vector.tensor_scalar(out=o[:, cols], in0=expd[b][:, cols], scalar1=r[:], scalar2=None, op0=ALU.mult)
                     queue.dma_start(out=out[rows, cols], in_=o[:, cols])
 
-        rotate(0)
-        combine(0)
-        rotate(1)
-        weave(0)
-        combine(1)
+        for part in range(2):
+            for b in range(EARLY):
+                heads[b, part] = project(b, part)
+        copy_y(0)
+        mul_y_ri(0)
+        mul_y_rr(0)
+        copy_y(1)
+        mul_e(0)
+        mul_y_rr(1)
+        mul_e(1)
+        mul_y_ri(1)
+        sub_z(0)
+        add_g(0)
+        sub_z(1)
         rotate(2)
+        round_g(0)
+        turn_g(0)
+        add_g(1)
+        weave_z(0)
+        weave_g(0)
         score(0)
-        weave(1)
+        weave_z(1)
+        round_g(1)
+        turn_g(1)
+        weave_g(1)
         combine(2)
         rotate(3)
         exponentiate(0)

@@ -102,7 +102,7 @@ def tile_picked_zcplx_soft_p_kernel(tc, x_words, x_scales, w1, w2, rr, ri, p_wor
         for t, c0 in ((rel0, 0), (rel1, P), (rel23, 2 * P)):
             for part in range(2):
                 load_relation(t, part, c0)
-        rel = [rel0[:], rel1[:], rel23[:, :, :, :P]]
+        rel = [rel0[:], rel1[:], rel23[:, :, :, :P], rel23[:, :, :, P:]]
 
         x_codes = gather_words("x_codes", xw_win, offs_t)
         x_sc = gather_scales("x_sc", xs_win, offs_t)
@@ -121,11 +121,6 @@ def tile_picked_zcplx_soft_p_kernel(tc, x_words, x_scales, w1, w2, rr, ri, p_wor
         w2_q = quantize_weight("w2", w2_grouped, "w2_codes")
         ident = keep.tile([P, P], F32, name="ident")
         make_identity(nc, ident[:])
-        woven = keep.tile([P, 2, P * PACK], F32, name="woven")
-        for part in range(2):
-            nc.scalar.copy(out=woven[:, part, :].rearrange("p (c i j) -> p c j i", i=4, j=PACK),
-                           in_=rel23[:, part, :, P:].rearrange("p j (c i) -> p c j i", i=4))
-        rel.append(woven[:].rearrange("p a (n j) -> p a n j", j=PACK))
 
         prod, sums, zg, bank, expd, total = {}, {}, {}, {}, {}, {}
         last = BLOCKS - 1
@@ -138,7 +133,7 @@ def tile_picked_zcplx_soft_p_kernel(tc, x_words, x_scales, w1, w2, rr, ri, p_wor
                 slot = slice(j * P, (j + 1) * P)
                 nc.tensor.matmul_mx(out=acc[:, j, :], lhsT=codes[:, slot].bitcast(FP8X4), lhsT_scale=scales[:, slot],
                                     rhs=x_codes[:, cols].bitcast(FP8X4), rhs_scale=x_sc[X_ROW:, cols], start=True, stop=True)
-            head = acc[:].rearrange("p j n -> p n j") if b == last else acc[:]
+            head = acc[:]
             if b >= EARLY:
                 prod[b, part] = keep.tile([P, 2] + list(head.shape[1:]), F32, name=f"prod{b}_{part}", align_bytes=64)
             return head
@@ -147,8 +142,11 @@ def tile_picked_zcplx_soft_p_kernel(tc, x_words, x_scales, w1, w2, rr, ri, p_wor
             y, e = project(b, 0), project(b, 1)
             if True:
                 nc.vector.tensor_tensor(out=prod[b, 0][:], in0=y.unsqueeze(1).to_broadcast(list(prod[b, 0].shape)), in1=rel[b], op=ALU.mult)
-            nc.vector.tensor_tensor(out=prod[b, 1][:, 1], in0=e, in1=rel[b][:, 0], op=ALU.mult)
-            nc.vector.scalar_tensor_tensor(out=prod[b, 1][:, 0], in0=e, scalar=-1.0, in1=rel[b][:, 1], op0=ALU.mult, op1=ALU.mult)
+            if b == last:
+                nc.vector.tensor_tensor(out=prod[b, 1][:], in0=e.unsqueeze(1).to_broadcast(list(prod[b, 1].shape)), in1=rel[b], op=ALU.mult)
+            else:
+                nc.vector.tensor_tensor(out=prod[b, 1][:, 1], in0=e, in1=rel[b][:, 0], op=ALU.mult)
+                nc.vector.scalar_tensor_tensor(out=prod[b, 1][:, 0], in0=e, scalar=-1.0, in1=rel[b][:, 1], op0=ALU.mult, op1=ALU.mult)
 
         def combine(b):
             t = laid.tile([P, 2, PACK, P], F32, name=f"sums{b}", align_bytes=64, offset=0)
@@ -208,7 +206,9 @@ def tile_picked_zcplx_soft_p_kernel(tc, x_words, x_scales, w1, w2, rr, ri, p_wor
             nc.scalar.copy(out=zg[b][:, 1, :].bitcast(F32).rearrange("p (n u) -> p n u", u=2), in_=g_words[b][:].rearrange("p u n -> p n u"))
 
         def combine_last(a):
-            nc.vector.tensor_tensor(out=zg[last][:, a].rearrange("p (n j) -> p n j", j=PACK), in0=prod[last, 0][:, a], in1=prod[last, 1][:, a], op=ALU.add)
+            pairs = "p j (c i) -> p c j i"
+            nc.vector.tensor_tensor(out=zg[last][:, a].rearrange("p (c i j) -> p c j i", i=2, j=PACK), in0=prod[last, 0][:, a].rearrange(pairs, i=2),
+                                    in1=prod[last, 1][:, (1, 0)[a]].rearrange(pairs, i=2), op=(ALU.subtract, ALU.add)[a])
 
         def score(b):
             codes = ring.tile([P, 2 * P], U32, name="zg_codes", align_bytes=64)

@@ -22,6 +22,11 @@ BLOCKS = PICKED // P
 HALF = 256
 X_ROW, P_ROW, Q_ROW = 4, 8, 12
 EARLY = 2
+OFFSET = {"y_ri0": 0, "w2_grouped0": 1024, "y_rr0": 2048, "y_rr1": 2048, "g_sum2": 4096, "zg0": 5120, "e_ri2": 6144}
+TAG = {"y_sb": "w2_raw1", "zg1": "y_ri1", "nmax3": "total1"}
+TURNED = ("bank_a", "bank_b")
+WORDS = ("bank_b", "bank_a")
+SCORES = ("bank_c", "bank_d", "bank_b", "bank_a")
 FLOPS = 4 * 2 * 512 * 512 * 512
 
 
@@ -51,12 +56,17 @@ def tile_picked_zcplx_soft_p_kernel(tc, x_words, x_scales, w1, w2, rr, ri, p_wor
             return t
 
         def load_weight(name, w, c0, width):
-            t = keep.tile([P, PACK, width], F32, name=name)
+            t = keep.tile([P, PACK, width], F32, name=name, align_bytes=64)
             nc.sync.dma_start(out=t[:], in_=w.rearrange("(p j) c -> p j c", j=PACK)[:, :, c0 : c0 + width])
             return t
 
         def load_relation(t, part, c0):
             nc.sync.dma_start(out=t[:, part], in_=(rr, ri)[part].rearrange("(p j) c -> p j c", j=PACK)[:, :, c0 : c0 + t.shape[3]])
+
+        def place(name, shape, dtype):
+            if name in OFFSET:
+                return laid.tile(shape, dtype, name=name, align_bytes=64, offset=OFFSET[name])
+            return keep.tile(shape, dtype, name=name, tag=TAG.get(name, name), align_bytes=64)
 
         def gather_words(name, window, offsets):
             t = keep.tile([P, PICKED], U32, name=name, align_bytes=64)
@@ -98,7 +108,7 @@ def tile_picked_zcplx_soft_p_kernel(tc, x_words, x_scales, w1, w2, rr, ri, p_wor
         w2_raw.append(load_weight("w2_raw1", w2, HALF, HALF))
         rel0 = keep.tile([P, 2, PACK, P], F32, name="rel0")
         rel1 = keep.tile([P, 2, PACK, P], F32, name="rel1")
-        rel23 = keep.tile([P, 2, PACK, 2 * P], F32, name="rel23")
+        rel23 = place("rel23", [P, 2, PACK, 2 * P], F32)
         for t, c0 in ((rel0, 0), (rel1, P), (rel23, 2 * P)):
             for part in range(2):
                 load_relation(t, part, c0)
@@ -113,7 +123,7 @@ def tile_picked_zcplx_soft_p_kernel(tc, x_words, x_scales, w1, w2, rr, ri, p_wor
         group(nc.scalar.copy, w1_grouped, w1_raw, 0, 1, 0, PACK)
         w1_q = quantize_weight("w1", [w1_grouped], "qw_win")
         q_sc = gather_scales("q_sc", qs_win, tail_t)
-        w2_grouped = [laid.tile([P, 2 * K], BF16, name=f"w2_grouped{h}", align_bytes=64, offset=(9216, 12288)[h]) for h in range(2)]
+        w2_grouped = [place(f"w2_grouped{h}", [P, 2 * K], BF16) for h in range(2)]
         group(nc.scalar.copy, w2_grouped[1], w2_raw[0], 0, 2, 2, 2)
         group(nc.scalar.copy, w2_grouped[0], w2_raw[0], 0, 2, 0, 2)
         group(nc.scalar.copy, w2_grouped[0], w2_raw[1], 1, 2, 0, 2)
@@ -122,8 +132,10 @@ def tile_picked_zcplx_soft_p_kernel(tc, x_words, x_scales, w1, w2, rr, ri, p_wor
         ident = keep.tile([P, P], F32, name="ident")
         make_identity(nc, ident[:])
 
-        prod, sums, zg, bank, expd, total = {}, {}, {}, {}, {}, {}
+        heads, y_rr, y_ri, e_rr, e_ri, z_sum, g_sum, g_turned, g_pairs, g_words = {}, {}, {}, {}, {}, {}, {}, {}, {}, {}
+        zg, quantised, bank, expd, total = {}, {}, {}, {}, {}
         last = BLOCKS - 1
+        y_sb = place("y_sb", [P, EARLY, PACK, P], F32)
 
         def project(b, part):
             codes, scales = (w1_q, w2_q)[part]
@@ -133,102 +145,92 @@ def tile_picked_zcplx_soft_p_kernel(tc, x_words, x_scales, w1, w2, rr, ri, p_wor
                 slot = slice(j * P, (j + 1) * P)
                 nc.tensor.matmul_mx(out=acc[:, j, :], lhsT=codes[:, slot].bitcast(FP8X4), lhsT_scale=scales[:, slot],
                                     rhs=x_codes[:, cols].bitcast(FP8X4), rhs_scale=x_sc[X_ROW:, cols], start=True, stop=True)
-            head = acc[:]
-            if b >= EARLY:
-                prod[b, part] = keep.tile([P, 2] + list(head.shape[1:]), F32, name=f"prod{b}_{part}", align_bytes=64)
-            return head
-
-        def rotate(b):
-            y, e = project(b, 0), project(b, 1)
-            if True:
-                nc.vector.tensor_tensor(out=prod[b, 0][:], in0=y.unsqueeze(1).to_broadcast(list(prod[b, 0].shape)), in1=rel[b], op=ALU.mult)
-            if b == last:
-                nc.vector.tensor_tensor(out=prod[b, 1][:], in0=e.unsqueeze(1).to_broadcast(list(prod[b, 1].shape)), in1=rel[b], op=ALU.mult)
-            else:
-                nc.vector.tensor_tensor(out=prod[b, 1][:, 1], in0=e, in1=rel[b][:, 0], op=ALU.mult)
-                nc.vector.scalar_tensor_tensor(out=prod[b, 1][:, 0], in0=e, scalar=-1.0, in1=rel[b][:, 1], op0=ALU.mult, op1=ALU.mult)
-
-        def combine(b):
-            t = laid.tile([P, 2, PACK, P], F32, name=f"sums{b}", align_bytes=64, offset=0)
-            if True:
-                nc.gpsimd.tensor_tensor(out=t[:], in0=prod[b, 0][:], in1=prod[b, 1][:], op=ALU.add)
-            sums[b] = t
-
-        def weave(b):
-            zg[b] = keep.tile([P, 2, P * PACK], BF16, name=f"zg{b}", align_bytes=64)
-            nc.scalar.copy(out=zg[b][:].rearrange("p a (c i j) -> p a c j i", i=4, j=PACK), in_=sums[b][:].rearrange("p a j (c i) -> p a c j i", i=4))
-
-        heads, y_rr, y_ri, e_r, z_sum, g_turned, g_pairs, g_words = {}, {}, {}, {}, {}, {}, {}, {}
-        y_sb = keep.tile([P, EARLY, PACK, P], F32, name="y_sb", tag="w2_raw1")
+            heads[b, part] = acc
 
         def copy_y(b):
-            nc.scalar.copy(out=y_sb[:, b], in_=heads[b, 0])
+            nc.scalar.copy(out=y_sb[:, b], in_=heads[b, 0][:])
 
         def mul_y_rr(b):
-            y_rr[b] = laid.tile([P, PACK, P], F32, name=f"y_rr{b}", align_bytes=64, offset=(10240, 16384)[b])
-            nc.gpsimd.tensor_tensor(out=y_rr[b][:], in0=y_sb[:, b], in1=rel[b][:, 0], op=ALU.mult)
+            t = place(f"y_rr{b}", [P, PACK, P], F32)
+            nc.gpsimd.tensor_tensor(out=t[:], in0=y_sb[:, b], in1=rel[b][:, 0], op=ALU.mult)
+            y_rr[b] = t[:]
 
-        def mul_y_ri(b):
-            y_ri[b] = laid.tile([P, PACK, P], F32, name=f"y_ri{b}", align_bytes=64, offset=(8192, 14336)[b])
-            nc.vector.tensor_tensor(out=y_ri[b][:], in0=heads[b, 0], in1=rel[b][:, 1], op=ALU.mult)
+        def mul_one(store, name, b, part, which):
+            t = place(f"{name}{b}", [P, PACK, P], F32)
+            nc.vector.tensor_tensor(out=t[:], in0=heads[b, part][:], in1=rel[b][:, which], op=ALU.mult)
+            store[b] = t[:]
 
-        def mul_e(b):
-            e_r[b] = keep.tile([P, 2, PACK, P], F32, name=f"e_r{b}")
-            nc.vector.tensor_tensor(out=e_r[b][:], in0=heads[b, 1].unsqueeze(1).to_broadcast([P, 2, PACK, P]), in1=rel[b], op=ALU.mult)
+        def mul_both(b, part):
+            t = place(f"prod{b}_{part}", [P, 2, PACK, P], F32)
+            nc.vector.tensor_tensor(out=t[:], in0=heads[b, part][:].unsqueeze(1).to_broadcast([P, 2, PACK, P]), in1=rel[b], op=ALU.mult)
+            with_rr, with_ri = ((y_rr, y_ri), (e_rr, e_ri))[part]
+            with_rr[b], with_ri[b] = t[:, 0], t[:, 1]
 
         def sub_z(b):
-            z_sum[b] = keep.tile([P, PACK, P], F32, name=f"z_sum{b}")
-            nc.gpsimd.tensor_tensor(out=z_sum[b][:], in0=y_rr[b][:], in1=e_r[b][:, 1], op=ALU.subtract)
+            z_sum[b] = place(f"z_sum{b}", [P, PACK, P], F32)
+            nc.gpsimd.tensor_tensor(out=z_sum[b][:], in0=y_rr[b], in1=e_ri[b], op=ALU.subtract)
 
-        def weave_z(b):
-            zg[b] = laid.tile([P, 2, P * PACK], BF16, name=f"zg{b}", align_bytes=64, offset=(2560, 4608)[b])
-            nc.scalar.copy(out=zg[b][:, 0, :].rearrange("p (c i j) -> p c j i", i=4, j=PACK), in_=z_sum[b][:].rearrange("p j (c i) -> p c j i", i=4))
+        def sum_g(b):
+            g_sum[b] = place(f"g_sum{b}", [P, PACK, P], F32)
+            nc.gpsimd.tensor_tensor(out=g_sum[b][:], in0=y_ri[b], in1=e_rr[b], op=ALU.add)
+
+        def zg_tile(b):
+            if b not in zg:
+                zg[b] = place(f"zg{b}", [P, 2, P * PACK], BF16)
+            return zg[b]
+
+        def weave(b, a):
+            nc.scalar.copy(out=zg_tile(b)[:, a, :].rearrange("p (c i j) -> p c j i", i=4, j=PACK), in_=(z_sum, g_sum)[a][b][:].rearrange("p j (c i) -> p c j i", i=4))
 
         def add_g(b):
-            acc = psum.tile([P, PACK, P], F32, name=f"g_turned{b}", tag="bank_a")
+            acc = psum.tile([P, PACK, P], F32, name=f"g_turned{b}", tag=TURNED[b])
             for j in range(PACK):
-                for term, src in enumerate((y_ri[b][:, j, :], e_r[b][:, 0, j, :])):
+                for term, src in enumerate((y_ri[b][:, j, :], e_rr[b][:, j, :])):
                     nc.tensor.matmul(acc[:, j, :], lhsT=src, rhs=ident[:], is_transpose=True, start=(term == 0), stop=(term == 1))
             g_turned[b] = acc
 
         def round_g(b):
-            g_pairs[b] = laid.tile([P, PACK * P], BF16, name=f"g_pairs{b}", align_bytes=64, offset=(4096, 6656)[b])
+            g_pairs[b] = place(f"g_pairs{b}", [P, PACK * P], BF16)
             nc.scalar.copy(out=g_pairs[b][:].rearrange("t (u p e) -> t u p e", u=2, e=2), in_=g_turned[b][:].rearrange("t (u e) p -> t u p e", e=2))
 
         def turn_g(b):
-            acc = psum.tile([P, 2, P], F32, name=f"g_words{b}", tag="bank_b")
+            acc = psum.tile([P, 2, P], F32, name=f"g_words{b}", tag=WORDS[b])
             words = g_pairs[b][:].bitcast(F32)
             for u in range(2):
                 nc.tensor.transpose(acc[:, u, :], words[:, u * P : (u + 1) * P], ident[:])
             g_words[b] = acc
 
         def weave_g(b):
-            nc.scalar.copy(out=zg[b][:, 1, :].bitcast(F32).rearrange("p (n u) -> p n u", u=2), in_=g_words[b][:].rearrange("p u n -> p n u"))
+            nc.scalar.copy(out=zg_tile(b)[:, 1, :].bitcast(F32).rearrange("p (n u) -> p n u", u=2), in_=g_words[b][:].rearrange("p u n -> p n u"))
 
         def combine_last(a):
             pairs = "p j (c i) -> p c j i"
-            nc.vector.tensor_tensor(out=zg[last][:, a].rearrange("p (c i j) -> p c j i", i=2, j=PACK), in0=prod[last, 0][:, a].rearrange(pairs, i=2),
-                                    in1=prod[last, 1][:, (1, 0)[a]].rearrange(pairs, i=2), op=(ALU.subtract, ALU.add)[a])
+            first, second = ((y_rr, e_ri), (y_ri, e_rr))[a]
+            nc.vector.tensor_tensor(out=zg_tile(last)[:, a].rearrange("p (c i j) -> p c j i", i=2, j=PACK), in0=first[last].rearrange(pairs, i=2),
+                                    in1=second[last].rearrange(pairs, i=2), op=(ALU.subtract, ALU.add)[a])
 
-        def score(b):
-            codes = ring.tile([P, 2 * P], U32, name="zg_codes", align_bytes=64)
-            scales = ring.tile([P, 2 * P], U8, name="zg_scales", align_bytes=64)
-            if b < BLOCKS - 1:
-                nc.vector.quantize_mx(out=codes[:].bitcast(FP8X4), scales=scales[:], in_=zg[b][:].rearrange("p a n -> p (a n)"))
-            acc = psum.tile([P, PICKED], F32, name=f"score{b}", tag=("bank_c", "bank_d", "bank_a", "bank_b")[b])
-            for which, (tail_codes, tail_scales) in enumerate(((p_codes[:], p_sc[P_ROW:, :]), (q_codes[:], q_sc[Q_ROW:, :]))):
-                cols = slice(which * P, (which + 1) * P)
-                if b == BLOCKS - 1:
-                    nc.vector.quantize_mx(out=codes[:, cols].bitcast(FP8X4), scales=scales[:, cols], in_=zg[b][:, which, :])
-                nc.tensor.matmul_mx(out=acc[:], lhsT=codes[:, cols].bitcast(FP8X4), lhsT_scale=scales[:, cols],
-                                    rhs=tail_codes.bitcast(FP8X4), rhs_scale=tail_scales, start=(which == 0), stop=(which == 1))
+        def quantise(b, halves):
+            width = len(halves) * P
+            codes = place(f"codes{b}_{halves[0]}", [P, width], U32)
+            scales = place(f"scales{b}_{halves[0]}", [P, width], U8)
+            nc.vector.quantize_mx(out=codes[:].bitcast(FP8X4), scales=scales[:], in_=zg[b][:, halves[0] : halves[-1] + 1].rearrange("p a n -> p (a n)"))
+            for n, a in enumerate(halves):
+                quantised[b, a] = codes[:, n * P : (n + 1) * P], scales[:, n * P : (n + 1) * P]
+
+        def score(b, order=(0, 1)):
+            acc = psum.tile([P, PICKED], F32, name=f"score{b}", tag=SCORES[b])
+            tails = ((p_codes[:], p_sc[P_ROW:, :]), (q_codes[:], q_sc[Q_ROW:, :]))
+            for n, a in enumerate(order):
+                codes, scales = quantised[b, a]
+                nc.tensor.matmul_mx(out=acc[:], lhsT=codes.bitcast(FP8X4), lhsT_scale=scales,
+                                    rhs=tails[a][0].bitcast(FP8X4), rhs_scale=tails[a][1], start=(n == 0), stop=(n == 1))
             bank[b] = acc
 
         def exponentiate(b):
-            m = keep.tile([P, 1], F32, name=f"nmax{b}", tag="total1" if b == last else f"nmax{b}")
+            m = place(f"nmax{b}", [P, 1], F32)
             nc.vector.tensor_reduce(out=m[:], in_=bank[b][:], axis=mybir.AxisListType.X, op=ALU.max, negate=True)
             e = ring.tile([P, PICKED], F32, name="expd")
-            s = keep.tile([P, 1], F32, name=f"total{b}")
+            s = place(f"total{b}", [P, 1], F32)
             nc.scalar.activation(out=e[:], in_=bank[b][:], func=ACT.Exp, bias=m[:], scale=1.0, accum_out=s[:])
             expd[b], total[b] = e, s
 
@@ -254,40 +256,54 @@ def tile_picked_zcplx_soft_p_kernel(tc, x_words, x_scales, w1, w2, rr, ri, p_wor
 
         for part in range(2):
             for b in range(EARLY):
-                heads[b, part] = project(b, part)
+                project(b, part)
         copy_y(0)
-        mul_y_ri(0)
+        mul_one(y_ri, "y_ri", 0, 0, 1)
         mul_y_rr(0)
         copy_y(1)
-        mul_e(0)
-        mul_y_rr(1)
-        mul_e(1)
-        mul_y_ri(1)
+        mul_one(e_ri, "e_ri", 0, 1, 1)
+        mul_one(e_rr, "e_rr", 0, 1, 0)
         sub_z(0)
+        mul_y_rr(1)
+        mul_both(1, 1)
+        mul_one(y_ri, "y_ri", 1, 0, 1)
         add_g(0)
         sub_z(1)
-        rotate(2)
+        project(2, 0)
+        project(2, 1)
+        weave(0, 0)
         round_g(0)
         turn_g(0)
-        add_g(1)
-        weave_z(0)
         weave_g(0)
+        mul_both(2, 0)
+        mul_one(e_rr, "e_rr", 2, 1, 0)
+        quantise(0, (0, 1))
+        mul_one(e_ri, "e_ri", 2, 1, 1)
+        project(3, 0)
+        project(3, 1)
+        add_g(1)
         score(0)
-        weave_z(1)
+        sum_g(2)
+        sub_z(2)
         round_g(1)
         turn_g(1)
+        weave(1, 0)
         weave_g(1)
-        combine(2)
-        rotate(3)
+        mul_both(3, 0)
+        mul_both(3, 1)
         exponentiate(0)
+        quantise(1, (0, 1))
         score(1)
-        weave(2)
-        zg[last] = keep.tile([P, 2, P * PACK], BF16, name="zg_last", align_bytes=64)
+        weave(2, 1)
+        weave(2, 0)
         combine_last(0)
         normalise(0)
+        quantise(2, (0, 1))
         score(2)
         combine_last(1)
         exponentiate(1)
+        quantise(3, (0,))
+        quantise(3, (1,))
         score(3)
         exponentiate(2)
         normalise(1)

@@ -206,8 +206,8 @@ def tile_picked_zcplx_soft_p_kernel(tc, x_words, x_scales, w1, w2, rr, ri, p_wor
         def combine_last(a):
             pairs = "p j (c i) -> p c j i"
             first, second = ((y_rr, e_ri), (y_ri, e_rr))[a]
-            nc.vector.tensor_tensor(out=zg_tile(last)[:, a].rearrange("p (c i j) -> p c j i", i=2, j=PACK), in0=first[last].rearrange(pairs, i=2),
-                                    in1=second[last].rearrange(pairs, i=2), op=(ALU.subtract, ALU.add)[a])
+            nc.vector.tensor_tensor(out=zg_tile(last)[:, a].rearrange("p (c i j) -> p c j i", i=4, j=PACK), in0=first[last].rearrange(pairs, i=4),
+                                    in1=second[last].rearrange(pairs, i=4), op=(ALU.subtract, ALU.add)[a])
 
         def quantise(b, halves):
             width = len(halves) * P

@@ -22,11 +22,11 @@ BLOCKS = PICKED // P
 HALF = 256
 X_ROW, P_ROW, Q_ROW = 4, 8, 12
 EARLY = 2
-OFFSET = {"y_ri0": 0, "w2_grouped0": 1024, "y_rr0": 2048, "y_rr1": 2048, "g_sum2": 4096, "zg0": 5120, "e_ri2": 6144}
+OFFSET = {"y_ri0": 0, "w2_grouped0": 1024, "y_rr0": 2048, "y_rr1": 2048, "g_sum2": 4096, "zg0": 5120, "prod_last": 6144}
 TAG = {"y_sb": "w2_raw1", "zg1": "y_ri1", "nmax3": "total1"}
-TURNED = ("bank_a", "bank_b")
-WORDS = ("bank_b", "bank_a")
-SCORES = ("bank_c", "bank_d", "bank_b", "bank_a")
+TURNED = ("bank_a", "bank_a")
+WORDS = ("bank_b", "bank_b")
+SCORES = ("bank_c", "bank_d", "bank_a", "bank_b")
 FLOPS = 4 * 2 * 512 * 512 * 512
 
 
@@ -110,7 +110,7 @@ def tile_picked_zcplx_soft_p_kernel(tc, x_words, x_scales, w1, w2, rr, ri, p_wor
         rel1 = keep.tile([P, 2, PACK, P], F32, name="rel1")
         rel23 = place("rel23", [P, 2, PACK, 2 * P], F32)
         for t, c0 in ((rel0, 0), (rel1, P), (rel23, 2 * P)):
-            for part in range(2):
+            for part in (1, 0) if c0 == 0 else (0, 1):
                 load_relation(t, part, c0)
         rel = [rel0[:], rel1[:], rel23[:, :, :, :P], rel23[:, :, :, P:]]
 
@@ -161,8 +161,8 @@ def tile_picked_zcplx_soft_p_kernel(tc, x_words, x_scales, w1, w2, rr, ri, p_wor
             store[b] = t[:]
 
         def mul_both(b, part):
-            t = place(f"prod{b}_{part}", [P, 2, PACK, P], F32)
-            nc.vector.tensor_tensor(out=t[:], in0=heads[b, part][:].unsqueeze(1).to_broadcast([P, 2, PACK, P]), in1=rel[b], op=ALU.mult)
+            t = prod_last[:, part] if b == last else place(f"prod{b}_{part}", [P, 2, PACK, P], F32)[:]
+            nc.vector.tensor_tensor(out=t, in0=heads[b, part][:].unsqueeze(1).to_broadcast([P, 2, PACK, P]), in1=rel[b], op=ALU.mult)
             with_rr, with_ri = ((y_rr, y_ri), (e_rr, e_ri))[part]
             with_rr[b], with_ri[b] = t[:, 0], t[:, 1]
 
@@ -274,14 +274,13 @@ def tile_picked_zcplx_soft_p_kernel(tc, x_words, x_scales, w1, w2, rr, ri, p_wor
         weave(0, 0)
         round_g(0)
         turn_g(0)
+        add_g(1)
         weave_g(0)
         mul_both(2, 0)
-        mul_one(e_rr, "e_rr", 2, 1, 0)
+        mul_both(2, 1)
         quantise(0, (0, 1))
-        mul_one(e_ri, "e_ri", 2, 1, 1)
         project(3, 0)
         project(3, 1)
-        add_g(1)
         score(0)
         sum_g(2)
         sub_z(2)
@@ -289,6 +288,7 @@ def tile_picked_zcplx_soft_p_kernel(tc, x_words, x_scales, w1, w2, rr, ri, p_wor
         turn_g(1)
         weave(1, 0)
         weave_g(1)
+        prod_last = place("prod_last", [P, 2, 2, PACK, P], F32)
         mul_both(3, 0)
         mul_both(3, 1)
         exponentiate(0)

@@ -22,11 +22,11 @@ BLOCKS = PICKED // P
 HALF = 256
 X_ROW, P_ROW, Q_ROW = 4, 8, 12
 EARLY = 2
-OFFSET = {"y_ri0": 0, "w2_grouped0": 1024, "y_rr0": 2048, "y_rr1": 2048, "g_sum2": 4096, "zg0": 5120, "prod_last": 6144}
-TAG = {"y_sb": "w2_raw1", "zg1": "y_ri1", "nmax3": "total1"}
-TURNED = ("bank_a", "bank_a")
-WORDS = ("bank_b", "bank_b")
-SCORES = ("bank_c", "bank_d", "bank_a", "bank_b")
+OFFSET = {"g_pairs0": 2048, "y_rr3": 0, "zg01": 1984, "z_sum2": 2048, "prod_last": 4096}
+TAG = {"y_sb": "w2_raw1", "codes2_0": "nmax0", "zg3": "total0", "codes3_0": "total1"}
+TURNED = ("bank_a", "bank_c")
+WORDS = ("bank_b", "bank_d")
+SCORES = ("bank_a", "bank_b", "bank_c", "bank_d")
 FLOPS = 4 * 2 * 512 * 512 * 512
 
 
@@ -34,7 +34,7 @@ def tile_picked_zcplx_soft_p_kernel(tc, x_words, x_scales, w1, w2, rr, ri, p_wor
     nc = tc.nc
     with ExitStack() as ctx:
         keep = ctx.enter_context(tc.tile_pool(name="keep", bufs=1))
-        ring = ctx.enter_context(tc.tile_pool(name="ring", bufs=3))
+        ring = ctx.enter_context(tc.tile_pool(name="ring", bufs=BLOCKS))
         laid = ctx.enter_context(tc.tile_pool(name="laid", bufs=1))
         psum = ctx.enter_context(tc.psum_pool(name="psum", bufs=1))
 
@@ -43,12 +43,20 @@ def tile_picked_zcplx_soft_p_kernel(tc, x_words, x_scales, w1, w2, rr, ri, p_wor
 
         def scale_window(name):
             t = keep.tile([P, TABLE], U8, name=name, align_bytes=64)
-            nc.vector.memset(t[:].bitcast(I32), 0)
+            nc.gpsimd.memset(t[:].bitcast(I32), 0)
             return t
 
-        def load_scales(t, src, first):
+        def load_scales(t, src):
+            nc.sync.dma_start(out=t[:16, :].bitcast(I32), in_=src[0].bitcast(I32))
+
+        def plane(name):
+            t = keep.tile([P, PICKED], U8, name=name, align_bytes=64)
+            nc.gpsimd.memset(t[:].bitcast(I32), 0)
+            return t
+
+        def spread(t, rows, first):
             for r in range(4):
-                nc.sync.dma_start(out=t[first + r : P : 32, :].bitcast(I32), in_=src[0, r:16:4, :].bitcast(I32))
+                nc.sync.dma_start(out=t[first + r : P : 32, :].bitcast(I32), in_=rows[r:16:4, :].bitcast(I32))
 
         def load_words(name, src):
             t = keep.tile([P, TABLE], I32, name=name, align_bytes=64)
@@ -95,34 +103,38 @@ def tile_picked_zcplx_soft_p_kernel(tc, x_words, x_scales, w1, w2, rr, ri, p_wor
         xs_win = scale_window("xs_win")
         ps_win = scale_window("ps_win")
         qs_win = scale_window("qs_win")
+        x_sc = plane("x_sc")
+        p_sc = plane("p_sc")
+        q_sc = plane("q_sc")
         nc.sync.dma_start(offs_t[:], offs)
+        load_scales(xs_win, x_scales)
         xw_win = load_words("xw_win", x_words)
-        load_scales(xs_win, x_scales, X_ROW)
-        w1_raw = load_weight("w1_raw", w1, 0, K)
         nc.sync.dma_start(tail_t[:], tail)
-        load_scales(ps_win, p_scales, P_ROW)
+        load_scales(ps_win, p_scales)
+        load_scales(qs_win, q_scales)
+        w1_raw = [load_weight(f"w1_raw{h}", w1, h * HALF, HALF) for h in range(2)]
+        x_rows = gather_scales("x_rows", xs_win, offs_t)
+        spread(x_sc, x_rows, X_ROW)
+        w2_raw = [load_weight(f"w2_raw{h}", w2, h * HALF, HALF) for h in range(2)]
+        rel01 = keep.tile([P, 2, PACK, HALF], F32, name="rel01")
+        rel23 = keep.tile([P, 2, PACK, HALF], F32, name="rel23")
+        load_relation(rel01, 1, 0)
+        load_relation(rel01, 0, 0)
         pw_win = load_words("pw_win", p_words)
+        load_relation(rel23, 0, HALF)
+        load_relation(rel23, 1, HALF)
         qw_win = load_words("qw_win", q_words)
-        w2_raw = [load_weight("w2_raw0", w2, 0, HALF)]
-        load_scales(qs_win, q_scales, Q_ROW)
-        w2_raw.append(load_weight("w2_raw1", w2, HALF, HALF))
-        rel0 = keep.tile([P, 2, PACK, P], F32, name="rel0")
-        rel1 = keep.tile([P, 2, PACK, P], F32, name="rel1")
-        rel23 = place("rel23", [P, 2, PACK, 2 * P], F32)
-        for t, c0 in ((rel0, 0), (rel1, P), (rel23, 2 * P)):
-            for part in (1, 0) if c0 == 0 else (0, 1):
-                load_relation(t, part, c0)
-        rel = [rel0[:], rel1[:], rel23[:, :, :, :P], rel23[:, :, :, P:]]
+        rel = [rel01[:, :, :, :P], rel01[:, :, :, P:], rel23[:, :, :, :P], rel23[:, :, :, P:]]
 
         x_codes = gather_words("x_codes", xw_win, offs_t)
-        x_sc = gather_scales("x_sc", xs_win, offs_t)
-        p_sc = gather_scales("p_sc", ps_win, tail_t)
-        p_codes = gather_words("p_codes", pw_win, tail_t)
-        q_codes = gather_words("q_codes", qw_win, tail_t)
+        p_rows = gather_scales("p_rows", ps_win, tail_t)
+        q_rows = gather_scales("q_rows", qs_win, tail_t)
+        spread(p_sc, p_rows, P_ROW)
+        spread(q_sc, q_rows, Q_ROW)
         w1_grouped = keep.tile([P, PACK * K], BF16, name="w1_grouped", align_bytes=64)
-        group(nc.scalar.copy, w1_grouped, w1_raw, 0, 1, 0, PACK)
-        w1_q = quantize_weight("w1", [w1_grouped], "qw_win")
-        q_sc = gather_scales("q_sc", qs_win, tail_t)
+        for h in range(2):
+            group(nc.scalar.copy, w1_grouped, w1_raw[h], h, 2, 0, PACK)
+        w1_q = quantize_weight("w1", [w1_grouped], "w1_codes")
         w2_grouped = [place(f"w2_grouped{h}", [P, 2 * K], BF16) for h in range(2)]
         group(nc.scalar.copy, w2_grouped[1], w2_raw[0], 0, 2, 2, 2)
         group(nc.scalar.copy, w2_grouped[0], w2_raw[0], 0, 2, 0, 2)
@@ -147,21 +159,24 @@ def tile_picked_zcplx_soft_p_kernel(tc, x_words, x_scales, w1, w2, rr, ri, p_wor
                                     rhs=x_codes[:, cols].bitcast(FP8X4), rhs_scale=x_sc[X_ROW:, cols], start=True, stop=True)
             heads[b, part] = acc
 
+        y_late = place("y_late", [P, PACK, P], F32)
+        y_copy = {0: y_sb[:, 0], 1: y_sb[:, 1], last: y_late[:]}
+
         def copy_y(b):
-            nc.scalar.copy(out=y_sb[:, b], in_=heads[b, 0][:])
+            nc.scalar.copy(out=y_copy[b], in_=heads[b, 0][:])
 
-        def mul_y_rr(b):
-            t = place(f"y_rr{b}", [P, PACK, P], F32)
-            nc.gpsimd.tensor_tensor(out=t[:], in0=y_sb[:, b], in1=rel[b][:, 0], op=ALU.mult)
-            y_rr[b] = t[:]
-
-        def mul_one(store, name, b, part, which):
+        def mul_y(store, name, b, which):
             t = place(f"{name}{b}", [P, PACK, P], F32)
-            nc.vector.tensor_tensor(out=t[:], in0=heads[b, part][:], in1=rel[b][:, which], op=ALU.mult)
+            nc.gpsimd.tensor_tensor(out=t[:], in0=y_copy[b], in1=rel[b][:, which], op=ALU.mult)
             store[b] = t[:]
 
+        def mul_one(store, name, b, part, which):
+            t = prod_last[:, 2] if b == last else place(f"{name}{b}", [P, PACK, P], F32)[:]
+            nc.vector.tensor_tensor(out=t, in0=heads[b, part][:], in1=rel[b][:, which], op=ALU.mult)
+            store[b] = t
+
         def mul_both(b, part):
-            t = prod_last[:, part] if b == last else place(f"prod{b}_{part}", [P, 2, PACK, P], F32)[:]
+            t = prod_last[:, :2] if b == last else place(f"prod{b}_{part}", [P, 2, PACK, P], F32)[:]
             nc.vector.tensor_tensor(out=t, in0=heads[b, part][:].unsqueeze(1).to_broadcast([P, 2, PACK, P]), in1=rel[b], op=ALU.mult)
             with_rr, with_ri = ((y_rr, y_ri), (e_rr, e_ri))[part]
             with_rr[b], with_ri[b] = t[:, 0], t[:, 1]
@@ -174,10 +189,20 @@ def tile_picked_zcplx_soft_p_kernel(tc, x_words, x_scales, w1, w2, rr, ri, p_wor
             g_sum[b] = place(f"g_sum{b}", [P, PACK, P], F32)
             nc.gpsimd.tensor_tensor(out=g_sum[b][:], in0=y_ri[b], in1=e_rr[b], op=ALU.add)
 
+
         def zg_tile(b):
             if b not in zg:
-                zg[b] = place(f"zg{b}", [P, 2, P * PACK], BF16)
+                zg[b] = place(f"zg{b}", [P, 2, P * PACK], BF16)[:]
             return zg[b]
+
+        def quantise_early():
+            codes = place("codes01", [P, 2 * EARLY * P], U32)
+            scales = place("scales01", [P, 2 * EARLY * P], U8)
+            nc.vector.quantize_mx(out=codes[:].bitcast(FP8X4), scales=scales[:], in_=zg01[:].rearrange("p b a n -> p (b a n)"))
+            for b in range(EARLY):
+                for a in range(2):
+                    cols = slice((2 * b + a) * P, (2 * b + a + 1) * P)
+                    quantised[b, a] = codes[:, cols], scales[:, cols]
 
         def weave(b, a):
             nc.scalar.copy(out=zg_tile(b)[:, a, :].rearrange("p (c i j) -> p c j i", i=4, j=PACK), in_=(z_sum, g_sum)[a][b][:].rearrange("p j (c i) -> p c j i", i=4))
@@ -239,11 +264,8 @@ def tile_picked_zcplx_soft_p_kernel(tc, x_words, x_scales, w1, w2, rr, ri, p_wor
             nc.vector.reciprocal(out=r[:], in_=total[b][:])
             rows = slice(b * P, (b + 1) * P)
             o = ring.tile([P, PICKED], F32, name="result")
-            if b == 0:
+            if b < EARLY:
                 nc.scalar.activation(out=o[:], in_=expd[b][:], func=ACT.Copy, scale=r[:])
-                nc.sync.dma_start(out=out[rows, :], in_=o[:])
-            elif b == 1:
-                nc.gpsimd.tensor_scalar(out=o[:], in0=expd[b][:], scalar1=r[:], scalar2=0.0, op0=ALU.mult, op1=ALU.add)
                 nc.sync.dma_start(out=out[rows, :], in_=o[:])
             elif b < last:
                 nc.vector.tensor_scalar(out=o[:], in0=expd[b][:], scalar1=r[:], scalar2=None, op0=ALU.mult)
@@ -258,55 +280,60 @@ def tile_picked_zcplx_soft_p_kernel(tc, x_words, x_scales, w1, w2, rr, ri, p_wor
             for b in range(EARLY):
                 project(b, part)
         copy_y(0)
-        mul_one(y_ri, "y_ri", 0, 0, 1)
-        mul_y_rr(0)
         copy_y(1)
+        mul_one(y_ri, "y_ri", 1, 0, 1)
+        mul_y(y_ri, "y_ri", 0, 1)
         mul_one(e_ri, "e_ri", 0, 1, 1)
         mul_one(e_rr, "e_rr", 0, 1, 0)
-        sub_z(0)
-        mul_y_rr(1)
-        mul_both(1, 1)
-        mul_one(y_ri, "y_ri", 1, 0, 1)
-        add_g(0)
-        sub_z(1)
+        mul_y(y_rr, "y_rr", 0, 0)
         project(2, 0)
-        project(2, 1)
-        weave(0, 0)
-        round_g(0)
-        turn_g(0)
-        add_g(1)
-        weave_g(0)
-        mul_both(2, 0)
-        mul_both(2, 1)
-        quantise(0, (0, 1))
         project(3, 0)
-        project(3, 1)
-        score(0)
-        sum_g(2)
-        sub_z(2)
+        copy_y(3)
+        project(2, 1)
+        mul_both(1, 1)
+        mul_y(y_rr, "y_rr", 1, 0)
+        sub_z(0)
+        add_g(0)
+        p_codes = gather_words("p_codes", pw_win, tail_t)
+        round_g(0)
+        add_g(1)
         round_g(1)
+        turn_g(0)
         turn_g(1)
-        weave(1, 0)
+        project(3, 1)
+        sub_z(1)
+        zg01 = place("zg01", [P, EARLY, 2, P * PACK], BF16)
+        zg[0], zg[1] = zg01[:, 0], zg01[:, 1]
+        weave(0, 0)
+        weave_g(0)
+        mul_both(2, 1)
+        mul_both(2, 0)
+        q_codes = gather_words("q_codes", qw_win, tail_t)
         weave_g(1)
-        prod_last = place("prod_last", [P, 2, 2, PACK, P], F32)
-        mul_both(3, 0)
-        mul_both(3, 1)
-        exponentiate(0)
-        quantise(1, (0, 1))
+        weave(1, 0)
+        sum_g(2)
+        quantise_early()
+        score(0)
         score(1)
         weave(2, 1)
+        prod_last = place("prod_last", [P, 3, PACK, P], F32)
+        sub_z(2)
+        mul_y(y_rr, "y_rr", 3, 0)
+        mul_one(y_ri, "y_ri", 3, 0, 1)
+        mul_both(3, 1)
         weave(2, 0)
-        combine_last(0)
+        exponentiate(0)
+        exponentiate(1)
         normalise(0)
         quantise(2, (0, 1))
         score(2)
+        combine_last(0)
+        normalise(1)
         combine_last(1)
-        exponentiate(1)
         quantise(3, (0,))
         quantise(3, (1,))
         score(3)
         exponentiate(2)
-        normalise(1)
         exponentiate(3)
         normalise(2)
         normalise(3)

@@ -20,12 +20,14 @@ TABLE = 1024
 PICKED = 512
 BLOCKS = PICKED // P
 HALF = 256
+SCALE_ROWS = 16
 X_ROW, P_ROW, Q_ROW = 4, 8, 12
-EARLY = 2
-OFFSET = {"g_pairs0": 2048, "y_rr3": 0, "zg01": 1984, "z_sum2": 2048, "prod_last": 4096}
-TAG = {"y_sb": "w2_raw1", "codes2_0": "nmax0", "zg3": "total0", "codes3_0": "total1"}
-TURNED = ("bank_a", "bank_c")
-WORDS = ("bank_b", "bank_d")
+RR, RI = 0, 1
+Y, E = 0, 1
+PIECES = ((0, 2, 0, HALF), (2, 4, 0, HALF), (0, 4, HALF, HALF + P), (0, 4, HALF + P, PICKED))
+OFFSET = {"g_pairs1": 0, "zg01": 0, "zg3": 0}
+TAG = {"dealt1_0": "dealt0_0", "y_both2": "y_rr1", "nmax2": "total0"}
+TURNED = ("bank_a", "bank_c", "bank_c")
 SCORES = ("bank_a", "bank_b", "bank_c", "bank_d")
 FLOPS = 4 * 2 * 512 * 512 * 512
 
@@ -34,238 +36,187 @@ def tile_picked_zcplx_soft_p_kernel(tc, x_words, x_scales, w1, w2, rr, ri, p_wor
     nc = tc.nc
     with ExitStack() as ctx:
         keep = ctx.enter_context(tc.tile_pool(name="keep", bufs=1))
-        ring = ctx.enter_context(tc.tile_pool(name="ring", bufs=BLOCKS))
         laid = ctx.enter_context(tc.tile_pool(name="laid", bufs=1))
         psum = ctx.enter_context(tc.psum_pool(name="psum", bufs=1))
 
         offs_t = keep.tile([P, PICKED // 16], U16, name="offs_t")
         tail_t = keep.tile([P, PICKED // 16], U16, name="tail_t")
 
-        def scale_window(name):
-            t = keep.tile([P, TABLE], U8, name=name, align_bytes=64)
-            nc.gpsimd.memset(t[:].bitcast(I32), 0)
-            return t
-
-        def load_scales(t, src):
-            nc.sync.dma_start(out=t[:16, :].bitcast(I32), in_=src[0].bitcast(I32))
-
-        def plane(name):
-            t = keep.tile([P, PICKED], U8, name=name, align_bytes=64)
-            nc.gpsimd.memset(t[:].bitcast(I32), 0)
-            return t
-
-        def spread(t, rows, first):
-            for r in range(4):
-                nc.sync.dma_start(out=t[first + r : P : 32, :].bitcast(I32), in_=rows[r:16:4, :].bitcast(I32))
-
-        def load_words(name, src):
-            t = keep.tile([P, TABLE], I32, name=name, align_bytes=64)
-            nc.sync.dma_start(out=t[:], in_=src[0].rearrange("p n t -> p (n t)").bitcast(I32))
-            return t
-
-        def load_weight(name, w, c0, width):
-            t = keep.tile([P, PACK, width], F32, name=name, align_bytes=64)
-            nc.sync.dma_start(out=t[:], in_=w.rearrange("(p j) c -> p j c", j=PACK)[:, :, c0 : c0 + width])
-            return t
-
-        def load_relation(t, part, c0):
-            nc.sync.dma_start(out=t[:, part], in_=(rr, ri)[part].rearrange("(p j) c -> p j c", j=PACK)[:, :, c0 : c0 + t.shape[3]])
-
         def place(name, shape, dtype):
             if name in OFFSET:
                 return laid.tile(shape, dtype, name=name, align_bytes=64, offset=OFFSET[name])
             return keep.tile(shape, dtype, name=name, tag=TAG.get(name, name), align_bytes=64)
 
-        def gather_words(name, window, offsets):
-            t = keep.tile([P, PICKED], U32, name=name, align_bytes=64)
-            nc.vector.tensor_copy(t[:], window[:].bitcast(U32).indirect(offsets[:]))
+        def cleared(name, width):
+            t = place(name, [P, width], U8)
+            nc.gpsimd.memset(t[:].bitcast(I32), 0)
             return t
 
-        def gather_scales(name, window, offsets):
-            t = keep.tile([P, PICKED], U8, name=name, align_bytes=64)
-            nc.vector.tensor_copy(t[:], window[:].indirect(offsets[:]))
+        def load_scales(t, src):
+            nc.sync.dma_start(out=t[:SCALE_ROWS, :].bitcast(I32), in_=src[0].bitcast(I32))
+
+        def spread(plane, rows, first):
+            for r in range(4):
+                nc.sync.dma_start(out=plane[first + r : P : 32, :].bitcast(I32), in_=rows[r:SCALE_ROWS:4, :].bitcast(I32))
+
+        def load_words(name, src):
+            t = place(name, [P, TABLE], I32)
+            nc.sync.dma_start(out=t[:], in_=src[0].rearrange("p n t -> p (n t)").bitcast(I32))
             return t
 
-        def group(copy, grouped, raw, piece, pieces, first, count):
-            span = P // pieces
-            copy(out=grouped[:].rearrange("p (t m j) -> p m j t", t=count, j=PACK)[:, span * piece : span * (piece + 1)],
-                 in_=raw[:].rearrange("p j (m t) -> p m j t", t=PACK)[:, :, :, first : first + count])
+        def load_weight(name, w):
+            t = place(name, [P, PACK, K], F32)
+            nc.sync.dma_start(out=t[:], in_=w.rearrange("(p j) c -> p j c", j=PACK))
+            return t
 
-        def quantize_weight(name, grouped, tag):
-            codes = keep.tile([P, K], U32, name=name + "_codes", tag=tag, align_bytes=64)
-            scales = keep.tile([P, K], U8, name=name + "_scales", align_bytes=64)
-            width = K // len(grouped)
-            for h in reversed(range(len(grouped))):
-                cols = slice(h * width, (h + 1) * width)
-                nc.vector.quantize_mx(out=codes[:, cols].bitcast(FP8X4), scales=scales[:, cols], in_=grouped[h][:])
-            return codes, scales
+        def load_relation(which, pair):
+            slots = slice(2 * pair, 2 * pair + 2)
+            nc.sync.dma_start(out=rel_t[:, which, slots], in_=(rr, ri)[which].rearrange("(p j) c -> p j c", j=PACK)[:, slots])
 
-        xs_win = scale_window("xs_win")
-        ps_win = scale_window("ps_win")
-        qs_win = scale_window("qs_win")
-        x_sc = plane("x_sc")
-        p_sc = plane("p_sc")
-        q_sc = plane("q_sc")
+        def gather(name, window, offsets, dtype):
+            t = place(name, [P, PICKED], dtype)
+            nc.vector.tensor_copy(t[:], window[:].bitcast(dtype).indirect(offsets[:]))
+            return t
+
+        def deal(copy, part, pair):
+            t = place(f"dealt{part}_{pair}", [P, 2 * K], BF16)
+            copy(out=t[:].rearrange("p (t m j) -> p m j t", t=2, j=PACK),
+                 in_=w_raw[part][:].rearrange("p j (m t) -> p m j t", t=PACK)[:, :, :, 2 * pair : 2 * pair + 2])
+            dealt[part, pair] = t
+
+        def quantise(name, values, width):
+            codes = place("codes" + name, [P, width], U32)
+            scales = place("scales" + name, [P, width], U8)
+            nc.vector.quantize_mx(out=codes[:].bitcast(FP8X4), scales=scales[:], in_=values)
+            return [(codes[:, c : c + P], scales[:, c : c + P]) for c in range(0, width, P)]
+
+        def quantise_weight(part, pair):
+            w_q[part, 2 * pair], w_q[part, 2 * pair + 1] = quantise(f"_w{part}_{pair}", dealt[part, pair][:], 2 * P)
+
+        dealt, w_q, heads, y_copy, prod, turned, pairs = {}, {}, {}, {}, {}, {}, {}
+        zg_q, bank, expd, total = {}, {}, {}, {}
+        last = BLOCKS - 1
+
+        xs_win, ps_win, qs_win = (cleared(name, TABLE) for name in ("xs_win", "ps_win", "qs_win"))
+        x_plane, p_plane, q_plane = (cleared(name, PICKED) for name in ("x_plane", "p_plane", "q_plane"))
         nc.sync.dma_start(offs_t[:], offs)
         load_scales(xs_win, x_scales)
         xw_win = load_words("xw_win", x_words)
         nc.sync.dma_start(tail_t[:], tail)
         load_scales(ps_win, p_scales)
         load_scales(qs_win, q_scales)
-        w1_raw = [load_weight(f"w1_raw{h}", w1, h * HALF, HALF) for h in range(2)]
-        x_rows = gather_scales("x_rows", xs_win, offs_t)
-        spread(x_sc, x_rows, X_ROW)
-        w2_raw = [load_weight(f"w2_raw{h}", w2, h * HALF, HALF) for h in range(2)]
-        rel01 = keep.tile([P, 2, PACK, HALF], F32, name="rel01")
-        rel23 = keep.tile([P, 2, PACK, HALF], F32, name="rel23")
-        load_relation(rel01, 1, 0)
-        load_relation(rel01, 0, 0)
+        w_raw = [load_weight("w1_raw", w1), load_weight("w2_raw", w2)]
+        x_rows = gather("x_rows", xs_win, offs_t, U8)
+        spread(x_plane, x_rows, X_ROW)
+        rel_t = place("rel_t", [P, 2, PACK, PICKED], F32)
+        for pair in range(2):
+            load_relation(RI, pair)
+            load_relation(RR, pair)
+        rel = [rel_t[:, :, j0:j1, c0:c1] for j0, j1, c0, c1 in PIECES]
         pw_win = load_words("pw_win", p_words)
-        load_relation(rel23, 0, HALF)
-        load_relation(rel23, 1, HALF)
         qw_win = load_words("qw_win", q_words)
-        rel = [rel01[:, :, :, :P], rel01[:, :, :, P:], rel23[:, :, :, :P], rel23[:, :, :, P:]]
 
-        x_codes = gather_words("x_codes", xw_win, offs_t)
-        p_rows = gather_scales("p_rows", ps_win, tail_t)
-        q_rows = gather_scales("q_rows", qs_win, tail_t)
-        spread(p_sc, p_rows, P_ROW)
-        spread(q_sc, q_rows, Q_ROW)
-        w1_grouped = keep.tile([P, PACK * K], BF16, name="w1_grouped", align_bytes=64)
-        for h in range(2):
-            group(nc.scalar.copy, w1_grouped, w1_raw[h], h, 2, 0, PACK)
-        w1_q = quantize_weight("w1", [w1_grouped], "w1_codes")
-        w2_grouped = [place(f"w2_grouped{h}", [P, 2 * K], BF16) for h in range(2)]
-        group(nc.scalar.copy, w2_grouped[1], w2_raw[0], 0, 2, 2, 2)
-        group(nc.scalar.copy, w2_grouped[0], w2_raw[0], 0, 2, 0, 2)
-        group(nc.scalar.copy, w2_grouped[0], w2_raw[1], 1, 2, 0, 2)
-        group(nc.vector.tensor_copy, w2_grouped[1], w2_raw[1], 1, 2, 2, 2)
-        w2_q = quantize_weight("w2", w2_grouped, "w2_codes")
+        x_codes = gather("x_codes", xw_win, offs_t, U32)
+        p_rows = gather("p_rows", ps_win, tail_t, U8)
+        q_rows = gather("q_rows", qs_win, tail_t, U8)
+        spread(p_plane, p_rows, P_ROW)
+        spread(q_plane, q_rows, Q_ROW)
+        deal(nc.scalar.copy, Y, 0)
+        deal(nc.scalar.copy, Y, 1)
+        quantise_weight(Y, 0)
+        deal(nc.vector.tensor_copy, E, 0)
+        deal(nc.scalar.copy, E, 1)
+        quantise_weight(Y, 1)
+        quantise_weight(E, 0)
+        quantise_weight(E, 1)
         ident = keep.tile([P, P], F32, name="ident")
         make_identity(nc, ident[:])
 
-        heads, y_rr, y_ri, e_rr, e_ri, z_sum, g_sum, g_turned, g_pairs, g_words = {}, {}, {}, {}, {}, {}, {}, {}, {}, {}
-        zg, quantised, bank, expd, total = {}, {}, {}, {}, {}
-        last = BLOCKS - 1
-        y_sb = place("y_sb", [P, EARLY, PACK, P], F32)
+        def shape_of(u):
+            j0, j1, c0, c1 = PIECES[u]
+            return [j1 - j0, c1 - c0]
 
-        def project(b, part):
-            codes, scales = (w1_q, w2_q)[part]
-            acc = psum.tile([P, PACK, P], F32, name=f"head{b}_{part}", tag=f"head{part}_{b % 2}")
-            cols = slice(b * P, (b + 1) * P)
-            for j in range(PACK):
-                slot = slice(j * P, (j + 1) * P)
-                nc.tensor.matmul_mx(out=acc[:, j, :], lhsT=codes[:, slot].bitcast(FP8X4), lhsT_scale=scales[:, slot],
-                                    rhs=x_codes[:, cols].bitcast(FP8X4), rhs_scale=x_sc[X_ROW:, cols], start=True, stop=True)
-            heads[b, part] = acc
+        def project(u, part):
+            j0, j1, c0, c1 = PIECES[u]
+            acc = psum.tile([P] + shape_of(u), F32, name=f"head{u}_{part}", tag=f"head{part}_{u % 2}")
+            for j in range(j0, j1):
+                codes, scales = w_q[part, j]
+                nc.tensor.matmul_mx(out=acc[:, j - j0, :], lhsT=codes.bitcast(FP8X4), lhsT_scale=scales,
+                                    rhs=x_codes[:, c0:c1].bitcast(FP8X4), rhs_scale=x_plane[X_ROW:, c0:c1], start=True, stop=True)
+            heads[u, part] = acc
 
-        y_late = place("y_late", [P, PACK, P], F32)
-        y_copy = {0: y_sb[:, 0], 1: y_sb[:, 1], last: y_late[:]}
+        def copy_y(u):
+            y_copy[u] = place(f"y_copy{u}", [P] + shape_of(u), F32)
+            nc.scalar.copy(out=y_copy[u][:], in_=heads[u, Y][:])
 
-        def copy_y(b):
-            nc.scalar.copy(out=y_copy[b], in_=heads[b, 0][:])
+        def mul_copy(u, which, dst=None):
+            if dst is None:
+                dst = place(f"y_{('rr', 'ri')[which]}{u}", [P] + shape_of(u), F32)[:]
+            nc.gpsimd.tensor_tensor(out=dst, in0=y_copy[u][:], in1=rel[u][:, which], op=ALU.mult)
+            prod[u, Y, which] = dst
 
-        def mul_y(store, name, b, which):
-            t = place(f"{name}{b}", [P, PACK, P], F32)
-            nc.gpsimd.tensor_tensor(out=t[:], in0=y_copy[b], in1=rel[b][:, which], op=ALU.mult)
-            store[b] = t[:]
+        def mul_bank(u, part, which):
+            t = place(f"prod{u}_{part}_{which}", [P] + shape_of(u), F32)
+            nc.vector.tensor_tensor(out=t[:], in0=heads[u, part][:], in1=rel[u][:, which], op=ALU.mult)
+            prod[u, part, which] = t[:]
 
-        def mul_one(store, name, b, part, which):
-            t = prod_last[:, 2] if b == last else place(f"{name}{b}", [P, PACK, P], F32)[:]
-            nc.vector.tensor_tensor(out=t, in0=heads[b, part][:], in1=rel[b][:, which], op=ALU.mult)
-            store[b] = t
+        def mul_both(u, part):
+            t = place(f"both{u}_{part}", [P, 2] + shape_of(u), F32)
+            nc.vector.tensor_tensor(out=t[:], in0=heads[u, part][:].unsqueeze(1).to_broadcast([P, 2] + shape_of(u)), in1=rel[u], op=ALU.mult)
+            prod[u, part, RR], prod[u, part, RI] = t[:, RR], t[:, RI]
 
-        def mul_both(b, part):
-            t = prod_last[:, :2] if b == last else place(f"prod{b}_{part}", [P, 2, PACK, P], F32)[:]
-            nc.vector.tensor_tensor(out=t, in0=heads[b, part][:].unsqueeze(1).to_broadcast([P, 2, PACK, P]), in1=rel[b], op=ALU.mult)
-            with_rr, with_ri = ((y_rr, y_ri), (e_rr, e_ri))[part]
-            with_rr[b], with_ri[b] = t[:, 0], t[:, 1]
+        def sub_z(u, dst):
+            nc.gpsimd.tensor_tensor(out=dst, in0=prod[u, Y, RR], in1=prod[u, E, RI], op=ALU.subtract)
 
-        def sub_z(b):
-            z_sum[b] = place(f"z_sum{b}", [P, PACK, P], F32)
-            nc.gpsimd.tensor_tensor(out=z_sum[b][:], in0=y_rr[b], in1=e_ri[b], op=ALU.subtract)
+        def weave(dst, src):
+            nc.scalar.copy(out=dst.rearrange("p (c i j) -> p c j i", i=4, j=PACK), in_=src.rearrange("p j (c i) -> p c j i", i=4))
 
-        def sum_g(b):
-            g_sum[b] = place(f"g_sum{b}", [P, PACK, P], F32)
-            nc.gpsimd.tensor_tensor(out=g_sum[b][:], in0=y_ri[b], in1=e_rr[b], op=ALU.add)
+        def add_g(u):
+            acc = psum.tile([P, PACK, P], F32, name=f"turned{u}", tag=TURNED[u])
+            for term, src in enumerate((prod[u, Y, RI], prod[u, E, RR])):
+                for n in range(PACK):
+                    block = src[:, n % 2, (n // 2) * P : (n // 2 + 1) * P] if u < 2 else src[:, n, :]
+                    nc.tensor.matmul(acc[:, n, :], lhsT=block, rhs=ident[:], is_transpose=True, start=(term == 0 and n == 0), stop=(term == 1 and n == PACK - 1))
+            turned[u] = acc
 
+        def round_g(u):
+            pairs[u] = place(f"g_pairs{u}", [P, PACK * P], BF16)
+            nc.scalar.copy(out=pairs[u][:].rearrange("t (h p e) -> t h p e", h=2, e=2), in_=turned[u][:].rearrange("t (h e) p -> t h p e", e=2))
 
-        def zg_tile(b):
-            if b not in zg:
-                zg[b] = place(f"zg{b}", [P, 2, P * PACK], BF16)[:]
-            return zg[b]
-
-        def quantise_early():
-            codes = place("codes01", [P, 2 * EARLY * P], U32)
-            scales = place("scales01", [P, 2 * EARLY * P], U8)
-            nc.vector.quantize_mx(out=codes[:].bitcast(FP8X4), scales=scales[:], in_=zg01[:].rearrange("p b a n -> p (b a n)"))
-            for b in range(EARLY):
-                for a in range(2):
-                    cols = slice((2 * b + a) * P, (2 * b + a + 1) * P)
-                    quantised[b, a] = codes[:, cols], scales[:, cols]
-
-        def weave(b, a):
-            nc.scalar.copy(out=zg_tile(b)[:, a, :].rearrange("p (c i j) -> p c j i", i=4, j=PACK), in_=(z_sum, g_sum)[a][b][:].rearrange("p j (c i) -> p c j i", i=4))
-
-        def add_g(b):
-            acc = psum.tile([P, PACK, P], F32, name=f"g_turned{b}", tag=TURNED[b])
-            for j in range(PACK):
-                for term, src in enumerate((y_ri[b][:, j, :], e_rr[b][:, j, :])):
-                    nc.tensor.matmul(acc[:, j, :], lhsT=src, rhs=ident[:], is_transpose=True, start=(term == 0), stop=(term == 1))
-            g_turned[b] = acc
-
-        def round_g(b):
-            g_pairs[b] = place(f"g_pairs{b}", [P, PACK * P], BF16)
-            nc.scalar.copy(out=g_pairs[b][:].rearrange("t (u p e) -> t u p e", u=2, e=2), in_=g_turned[b][:].rearrange("t (u e) p -> t u p e", e=2))
-
-        def turn_g(b):
-            acc = psum.tile([P, 2, P], F32, name=f"g_words{b}", tag=WORDS[b])
-            words = g_pairs[b][:].bitcast(F32)
-            for u in range(2):
-                nc.tensor.transpose(acc[:, u, :], words[:, u * P : (u + 1) * P], ident[:])
-            g_words[b] = acc
-
-        def weave_g(b):
-            nc.scalar.copy(out=zg_tile(b)[:, 1, :].bitcast(F32).rearrange("p (n u) -> p n u", u=2), in_=g_words[b][:].rearrange("p u n -> p n u"))
+        def turn_g(u, dst):
+            words = pairs[u][:].bitcast(F32)
+            for h in range(2):
+                nc.tensor.transpose(dst[:, h, :], words[:, h * P : (h + 1) * P], ident[:])
 
         def combine_last(a):
-            pairs = "p j (c i) -> p c j i"
-            first, second = ((y_rr, e_ri), (y_ri, e_rr))[a]
-            nc.vector.tensor_tensor(out=zg_tile(last)[:, a].rearrange("p (c i j) -> p c j i", i=4, j=PACK), in0=first[last].rearrange(pairs, i=4),
-                                    in1=second[last].rearrange(pairs, i=4), op=(ALU.subtract, ALU.add)[a])
+            walk = "p j (c i) -> p c j i"
+            first, second = ((RR, RI), (RI, RR))[a]
+            nc.vector.tensor_tensor(out=zg3[:, a].rearrange("p (c i j) -> p c j i", i=4, j=PACK), in0=prod[last, Y, first].rearrange(walk, i=4),
+                                    in1=prod[last, E, second].rearrange(walk, i=4), op=(ALU.subtract, ALU.add)[a])
 
-        def quantise(b, halves):
-            width = len(halves) * P
-            codes = place(f"codes{b}_{halves[0]}", [P, width], U32)
-            scales = place(f"scales{b}_{halves[0]}", [P, width], U8)
-            nc.vector.quantize_mx(out=codes[:].bitcast(FP8X4), scales=scales[:], in_=zg[b][:, halves[0] : halves[-1] + 1].rearrange("p a n -> p (a n)"))
-            for n, a in enumerate(halves):
-                quantised[b, a] = codes[:, n * P : (n + 1) * P], scales[:, n * P : (n + 1) * P]
-
-        def score(b, order=(0, 1)):
+        def score(b):
             acc = psum.tile([P, PICKED], F32, name=f"score{b}", tag=SCORES[b])
-            tails = ((p_codes[:], p_sc[P_ROW:, :]), (q_codes[:], q_sc[Q_ROW:, :]))
-            for n, a in enumerate(order):
-                codes, scales = quantised[b, a]
+            tails = ((p_codes[:], p_plane[P_ROW:, :]), (q_codes[:], q_plane[Q_ROW:, :]))
+            for a in range(2):
+                codes, scales = zg_q[b, a]
                 nc.tensor.matmul_mx(out=acc[:], lhsT=codes.bitcast(FP8X4), lhsT_scale=scales,
-                                    rhs=tails[a][0].bitcast(FP8X4), rhs_scale=tails[a][1], start=(n == 0), stop=(n == 1))
+                                    rhs=tails[a][0].bitcast(FP8X4), rhs_scale=tails[a][1], start=(a == 0), stop=(a == 1))
             bank[b] = acc
 
         def exponentiate(b):
             m = place(f"nmax{b}", [P, 1], F32)
             nc.vector.tensor_reduce(out=m[:], in_=bank[b][:], axis=mybir.AxisListType.X, op=ALU.max, negate=True)
-            e = ring.tile([P, PICKED], F32, name="expd")
-            s = place(f"total{b}", [P, 1], F32)
-            nc.scalar.activation(out=e[:], in_=bank[b][:], func=ACT.Exp, bias=m[:], scale=1.0, accum_out=s[:])
-            expd[b], total[b] = e, s
+            expd[b] = place(f"expd{b}", [P, PICKED], F32)
+            total[b] = place(f"total{b}", [P, 1], F32)
+            nc.scalar.activation(out=expd[b][:], in_=bank[b][:], func=ACT.Exp, bias=m[:], scale=1.0, accum_out=total[b][:])
 
         def normalise(b):
-            r = ring.tile([P, 1], F32, name="recip")
+            r = place(f"recip{b}", [P, 1], F32)
             nc.vector.reciprocal(out=r[:], in_=total[b][:])
             rows = slice(b * P, (b + 1) * P)
-            o = ring.tile([P, PICKED], F32, name="result")
-            if b < EARLY:
-                nc.scalar.activation(out=o[:], in_=expd[b][:], func=ACT.Copy, scale=r[:])
+            o = place(f"result{b}", [P, PICKED], F32)
+            if b == 0:
+                nc.gpsimd.tensor_scalar(out=o[:], in0=expd[b][:], scalar1=r[:], scalar2=0.0, op0=ALU.mult, op1=ALU.add)
                 nc.sync.dma_start(out=out[rows, :], in_=o[:])
             elif b < last:
                 nc.vector.tensor_scalar(out=o[:], in0=expd[b][:], scalar1=r[:], scalar2=None, op0=ALU.mult)
@@ -276,64 +227,69 @@ def tile_picked_zcplx_soft_p_kernel(tc, x_words, x_scales, w1, w2, rr, ri, p_wor
                     nc.vector.tensor_scalar(out=o[:, cols], in0=expd[b][:, cols], scalar1=r[:], scalar2=None, op0=ALU.mult)
                     queue.dma_start(out=out[rows, cols], in_=o[:, cols])
 
-        for part in range(2):
-            for b in range(EARLY):
-                project(b, part)
+        project(0, Y)
+        project(0, E)
+        project(1, Y)
+        project(1, E)
         copy_y(0)
         copy_y(1)
-        mul_one(y_ri, "y_ri", 1, 0, 1)
-        mul_y(y_ri, "y_ri", 0, 1)
-        mul_one(e_ri, "e_ri", 0, 1, 1)
-        mul_one(e_rr, "e_rr", 0, 1, 0)
-        mul_y(y_rr, "y_rr", 0, 0)
-        project(2, 0)
-        project(3, 0)
-        copy_y(3)
-        project(2, 1)
-        mul_both(1, 1)
-        mul_y(y_rr, "y_rr", 1, 0)
-        sub_z(0)
+        mul_bank(0, Y, RI)
+        mul_bank(0, E, RI)
+        mul_copy(0, RR)
+        mul_bank(0, E, RR)
+        project(2, Y)
+        project(2, E)
+        copy_y(2)
+        z01 = place("z01", [P, PACK, HALF], F32)
+        sub_z(0, z01[:, :2])
+        mul_bank(1, Y, RI)
+        mul_bank(1, E, RI)
+        mul_bank(1, E, RR)
+        mul_copy(1, RR)
         add_g(0)
-        p_codes = gather_words("p_codes", pw_win, tail_t)
         round_g(0)
         add_g(1)
         round_g(1)
-        turn_g(0)
-        turn_g(1)
-        project(3, 1)
-        sub_z(1)
-        zg01 = place("zg01", [P, EARLY, 2, P * PACK], BF16)
-        zg[0], zg[1] = zg01[:, 0], zg01[:, 1]
-        weave(0, 0)
-        weave_g(0)
-        mul_both(2, 1)
-        mul_both(2, 0)
-        q_codes = gather_words("q_codes", qw_win, tail_t)
-        weave_g(1)
-        weave(1, 0)
-        sum_g(2)
-        quantise_early()
+        words01 = psum.tile([P, 2, 2, P], F32, name="words01", tag="bank_b")
+        turn_g(0, words01[:, :, 0])
+        turn_g(1, words01[:, :, 1])
+        project(3, Y)
+        project(3, E)
+        sub_z(1, z01[:, 2:])
+        mul_both(2, E)
+        zg01 = place("zg01", [P, 2, HALF * PACK], BF16)
+        nc.scalar.copy(out=zg01[:, 1].bitcast(F32).rearrange("p (b n h) -> p b n h", b=2, h=2), in_=words01[:].rearrange("p b h n -> p b n h"))
+        weave(zg01[:, 0], z01[:])
+        p_codes = gather("p_codes", pw_win, tail_t, U32)
+        q_codes = gather("q_codes", qw_win, tail_t, U32)
+        mul_both(3, Y)
+        mul_both(3, E)
+        y_both2 = place("y_both2", [P, 2, PACK, P], F32)
+        mul_copy(2, RI, y_both2[:, RI])
+        mul_copy(2, RR, y_both2[:, RR])
+        add_g(2)
+        round_g(2)
+        zg_q[0, 0], zg_q[1, 0], zg_q[0, 1], zg_q[1, 1] = quantise("01", zg01[:].rearrange("p a n -> p (a n)"), 4 * P)
         score(0)
+        words2 = psum.tile([P, 2, P], F32, name="words2", tag="bank_d")
+        turn_g(2, words2)
         score(1)
-        weave(2, 1)
-        prod_last = place("prod_last", [P, 3, PACK, P], F32)
-        sub_z(2)
-        mul_y(y_rr, "y_rr", 3, 0)
-        mul_one(y_ri, "y_ri", 3, 0, 1)
-        mul_both(3, 1)
-        weave(2, 0)
+        zg2 = place("zg2", [P, 2, P * PACK], BF16)
+        nc.scalar.copy(out=zg2[:, 1].bitcast(F32).rearrange("p (n h) -> p n h", h=2), in_=words2[:].rearrange("p h n -> p n h"))
+        z_sum2 = place("z_sum2", [P, PACK, P], F32)
+        sub_z(2, z_sum2[:])
+        weave(zg2[:, 0], z_sum2[:])
+        zg3 = place("zg3", [P, 2, P * PACK], BF16)
+        combine_last(0)
+        combine_last(1)
+        zg_q[2, 0], zg_q[2, 1] = quantise("2", zg2[:].rearrange("p a n -> p (a n)"), 2 * P)
+        score(2)
+        zg_q[last, 0], zg_q[last, 1] = quantise("3", zg3[:].rearrange("p a n -> p (a n)"), 2 * P)
+        score(3)
         exponentiate(0)
         exponentiate(1)
         normalise(0)
-        quantise(2, (0, 1))
-        score(2)
-        combine_last(0)
-        normalise(1)
-        combine_last(1)
-        quantise(3, (0,))
-        quantise(3, (1,))
-        score(3)
         exponentiate(2)
         exponentiate(3)
-        normalise(2)
-        normalise(3)
+        for b in range(1, BLOCKS):
+            normalise(b)

@@ -119,8 +119,8 @@ def tile_picked_zcplx_soft_p_kernel(tc, x_words, x_scales, w1, w2, rr, ri, p_wor
         x_codes = gather("x_codes", xw_win, offs_t, U32)
         p_rows = gather("p_rows", ps_win, tail_t, U8)
         q_rows = gather("q_rows", qs_win, tail_t, U8)
-        spread(p_plane, p_rows, P_ROW)
         spread(q_plane, q_rows, Q_ROW)
+        spread(p_plane, p_rows, P_ROW)
         deal(nc.scalar.copy, Y, 0)
         deal(nc.scalar.copy, Y, 1)
         quantise_weight(Y, 0)
@@ -269,10 +269,10 @@ def tile_picked_zcplx_soft_p_kernel(tc, x_words, x_scales, w1, w2, rr, ri, p_wor
         mul_copy(2, RR, y_both2[:, RR])
         add_g(2)
         round_g(2)
-        zg_q[0, 0], zg_q[1, 0], zg_q[0, 1], zg_q[1, 1] = quantise("01", zg01[:].rearrange("p a n -> p (a n)"), 4 * P)
-        score(0)
         words2 = psum.tile([P, 2, P], F32, name="words2", tag="bank_d")
         turn_g(2, words2)
+        zg_q[0, 0], zg_q[1, 0], zg_q[0, 1], zg_q[1, 1] = quantise("01", zg01[:].rearrange("p a n -> p (a n)"), 4 * P)
+        score(0)
         score(1)
         zg2 = place("zg2", [P, 2, P * PACK], BF16)
         nc.scalar.copy(out=zg2[:, 1].bitcast(F32).rearrange("p (n h) -> p n h", h=2), in_=words2[:].rearrange("p h n -> p n h"))
@@ -282,11 +282,11 @@ def tile_picked_zcplx_soft_p_kernel(tc, x_words, x_scales, w1, w2, rr, ri, p_wor
         zg3 = place("zg3", [P, 2, P * PACK], BF16)
         combine_last(0)
         combine_last(1)
+        exponentiate(0)
         zg_q[2, 0], zg_q[2, 1] = quantise("2", zg2[:].rearrange("p a n -> p (a n)"), 2 * P)
         score(2)
         zg_q[last, 0], zg_q[last, 1] = quantise("3", zg3[:].rearrange("p a n -> p (a n)"), 2 * P)
         score(3)
-        exponentiate(0)
         exponentiate(1)
         normalise(0)
         exponentiate(2)

@@ -25,8 +25,8 @@ X_ROW, P_ROW, Q_ROW = 4, 8, 12
 RR, RI = 0, 1
 Y, E = 0, 1
 PIECES = ((0, 2, 0, HALF), (2, 4, 0, HALF), (0, 4, HALF, HALF + P), (0, 4, HALF + P, PICKED))
-OFFSET = {"g_pairs1": 0, "zg01": 0, "zg3": 0}
-TAG = {"dealt1_0": "dealt0_0", "y_both2": "y_rr1", "nmax2": "total0"}
+OFFSET = {"g_pairs1": 0, "zg01": 0, "zg3": 0, "z01": 4096, "zg2": 4096, "g_pairs2": 6144}
+TAG = {"dealt1_0": "dealt0_0", "nmax2": "total0"}
 TURNED = ("bank_a", "bank_c", "bank_c")
 SCORES = ("bank_a", "bank_b", "bank_c", "bank_d")
 FLOPS = 4 * 2 * 512 * 512 * 512
@@ -241,19 +241,21 @@ def tile_picked_zcplx_soft_p_kernel(tc, x_words, x_scales, w1, w2, rr, ri, p_wor
         project(2, E)
         copy_y(2)
         z01 = place("z01", [P, PACK, HALF], F32)
+        mul_copy(1, RI)
         sub_z(0, z01[:, :2])
-        mul_bank(1, Y, RI)
         mul_bank(1, E, RI)
+        mul_bank(2, Y, RI)
         mul_bank(1, E, RR)
-        mul_copy(1, RR)
+        mul_bank(1, Y, RR)
         add_g(0)
         round_g(0)
         add_g(1)
         round_g(1)
+        project(3, Y)
+        copy_y(3)
         words01 = psum.tile([P, 2, 2, P], F32, name="words01", tag="bank_b")
         turn_g(0, words01[:, :, 0])
         turn_g(1, words01[:, :, 1])
-        project(3, Y)
         project(3, E)
         sub_z(1, z01[:, 2:])
         mul_both(2, E)
@@ -262,11 +264,12 @@ def tile_picked_zcplx_soft_p_kernel(tc, x_words, x_scales, w1, w2, rr, ri, p_wor
         weave(zg01[:, 0], z01[:])
         p_codes = gather("p_codes", pw_win, tail_t, U32)
         q_codes = gather("q_codes", qw_win, tail_t, U32)
-        mul_both(3, Y)
+        mul_bank(3, Y, RI)
         mul_both(3, E)
-        y_both2 = place("y_both2", [P, 2, PACK, P], F32)
-        mul_copy(2, RI, y_both2[:, RI])
-        mul_copy(2, RR, y_both2[:, RR])
+        mul_copy(2, RR)
+        mul_copy(3, RR)
+        z_sum2 = place("z_sum2", [P, PACK, P], F32)
+        sub_z(2, z_sum2[:])
         add_g(2)
         round_g(2)
         words2 = psum.tile([P, 2, P], F32, name="words2", tag="bank_d")
@@ -276,8 +279,6 @@ def tile_picked_zcplx_soft_p_kernel(tc, x_words, x_scales, w1, w2, rr, ri, p_wor
         score(1)
         zg2 = place("zg2", [P, 2, P * PACK], BF16)
         nc.scalar.copy(out=zg2[:, 1].bitcast(F32).rearrange("p (n h) -> p n h", h=2), in_=words2[:].rearrange("p h n -> p n h"))
-        z_sum2 = place("z_sum2", [P, PACK, P], F32)
-        sub_z(2, z_sum2[:])
         weave(zg2[:, 0], z_sum2[:])
         zg3 = place("zg3", [P, 2, P * PACK], BF16)
         combine_last(0)

@@ -14,18 +14,19 @@ ALU = mybir.AluOpType
 ACT = mybir.ActivationFunctionType
 
 P = 128
-PACK = 4
-K = 512
+SLOTS = 4
+HIDDEN = 512
 TABLE = 1024
 PICKED = 512
-BLOCKS = PICKED // P
-HALF = 256
+HALF = PICKED // 2
+LAST = PICKED // P - 1
 SCALE_ROWS = 16
+RUN = 4
 X_ROW, P_ROW, Q_ROW = 4, 8, 12
 RR, RI = 0, 1
 Y, E = 0, 1
 PIECES = ((0, 2, 0, HALF), (2, 4, 0, HALF), (0, 4, HALF, HALF + P), (0, 4, HALF + P, PICKED))
-OFFSET = {"g_pairs1": 0, "zg01": 0, "zg3": 0, "z01": 4096, "zg2": 4096, "g_pairs2": 6144}
+SHARED = ("g_pairs1", "zg01", "zg3")
 TAG = {"dealt1_0": "dealt0_0", "nmax2": "total0"}
 TURNED = ("bank_a", "bank_c", "bank_c")
 SCORES = ("bank_a", "bank_b", "bank_c", "bank_d")
@@ -36,15 +37,15 @@ def tile_picked_zcplx_soft_p_kernel(tc, x_words, x_scales, w1, w2, rr, ri, p_wor
     nc = tc.nc
     with ExitStack() as ctx:
         keep = ctx.enter_context(tc.tile_pool(name="keep", bufs=1))
-        laid = ctx.enter_context(tc.tile_pool(name="laid", bufs=1))
+        shared = ctx.enter_context(tc.tile_pool(name="shared", bufs=1))
         psum = ctx.enter_context(tc.psum_pool(name="psum", bufs=1))
 
         offs_t = keep.tile([P, PICKED // 16], U16, name="offs_t")
         tail_t = keep.tile([P, PICKED // 16], U16, name="tail_t")
 
         def place(name, shape, dtype):
-            if name in OFFSET:
-                return laid.tile(shape, dtype, name=name, align_bytes=64, offset=OFFSET[name])
+            if name in SHARED:
+                return shared.tile(shape, dtype, name=name, align_bytes=64, offset=0)
             return keep.tile(shape, dtype, name=name, tag=TAG.get(name, name), align_bytes=64)
 
         def cleared(name, width):
@@ -52,8 +53,8 @@ def tile_picked_zcplx_soft_p_kernel(tc, x_words, x_scales, w1, w2, rr, ri, p_wor
             nc.gpsimd.memset(t[:].bitcast(I32), 0)
             return t
 
-        def load_scales(t, src):
-            nc.sync.dma_start(out=t[:SCALE_ROWS, :].bitcast(I32), in_=src[0].bitcast(I32))
+        def load_scales(window, src):
+            nc.sync.dma_start(out=window[:SCALE_ROWS, :].bitcast(I32), in_=src[0].bitcast(I32))
 
         def spread(plane, rows, first):
             for r in range(4):
@@ -65,13 +66,13 @@ def tile_picked_zcplx_soft_p_kernel(tc, x_words, x_scales, w1, w2, rr, ri, p_wor
             return t
 
         def load_weight(name, w):
-            t = place(name, [P, PACK, K], F32)
-            nc.sync.dma_start(out=t[:], in_=w.rearrange("(p j) c -> p j c", j=PACK))
+            t = place(name, [P, SLOTS, HIDDEN], F32)
+            nc.sync.dma_start(out=t[:], in_=w.rearrange("(p j) c -> p j c", j=SLOTS))
             return t
 
         def load_relation(which, pair):
             slots = slice(2 * pair, 2 * pair + 2)
-            nc.sync.dma_start(out=rel_t[:, which, slots], in_=(rr, ri)[which].rearrange("(p j) c -> p j c", j=PACK)[:, slots])
+            nc.sync.dma_start(out=rel_t[:, which, slots], in_=(rr, ri)[which].rearrange("(p j) c -> p j c", j=SLOTS)[:, slots])
 
         def gather(name, window, offsets, dtype):
             t = place(name, [P, PICKED], dtype)
@@ -79,9 +80,9 @@ def tile_picked_zcplx_soft_p_kernel(tc, x_words, x_scales, w1, w2, rr, ri, p_wor
             return t
 
         def deal(copy, part, pair):
-            t = place(f"dealt{part}_{pair}", [P, 2 * K], BF16)
-            copy(out=t[:].rearrange("p (t m j) -> p m j t", t=2, j=PACK),
-                 in_=w_raw[part][:].rearrange("p j (m t) -> p m j t", t=PACK)[:, :, :, 2 * pair : 2 * pair + 2])
+            t = place(f"dealt{part}_{pair}", [P, 2 * P * SLOTS], BF16)
+            copy(out=t[:].rearrange("p (t m j) -> p m j t", t=2, j=SLOTS),
+                 in_=w_raw[part][:].rearrange("p j (m t) -> p m j t", t=SLOTS)[:, :, :, 2 * pair : 2 * pair + 2])
             dealt[part, pair] = t
 
         def quantise(name, values, width):
@@ -94,8 +95,7 @@ def tile_picked_zcplx_soft_p_kernel(tc, x_words, x_scales, w1, w2, rr, ri, p_wor
             w_q[part, 2 * pair], w_q[part, 2 * pair + 1] = quantise(f"_w{part}_{pair}", dealt[part, pair][:], 2 * P)
 
         dealt, w_q, heads, y_copy, prod, turned, pairs = {}, {}, {}, {}, {}, {}, {}
-        zg_q, bank, expd, total = {}, {}, {}, {}
-        last = BLOCKS - 1
+        zg_q, bank, expd, total, recip = {}, {}, {}, {}, {}
 
         xs_win, ps_win, qs_win = (cleared(name, TABLE) for name in ("xs_win", "ps_win", "qs_win"))
         x_plane, p_plane, q_plane = (cleared(name, PICKED) for name in ("x_plane", "p_plane", "q_plane"))
@@ -108,7 +108,7 @@ def tile_picked_zcplx_soft_p_kernel(tc, x_words, x_scales, w1, w2, rr, ri, p_wor
         w_raw = [load_weight("w1_raw", w1), load_weight("w2_raw", w2)]
         x_rows = gather("x_rows", xs_win, offs_t, U8)
         spread(x_plane, x_rows, X_ROW)
-        rel_t = place("rel_t", [P, 2, PACK, PICKED], F32)
+        rel_t = place("rel_t", [P, 2, SLOTS, PICKED], F32)
         for pair in range(2):
             load_relation(RI, pair)
             load_relation(RR, pair)
@@ -149,38 +149,37 @@ def tile_picked_zcplx_soft_p_kernel(tc, x_words, x_scales, w1, w2, rr, ri, p_wor
             y_copy[u] = place(f"y_copy{u}", [P] + shape_of(u), F32)
             nc.scalar.copy(out=y_copy[u][:], in_=heads[u, Y][:])
 
-        def mul_copy(u, which, dst=None):
-            if dst is None:
-                dst = place(f"y_{('rr', 'ri')[which]}{u}", [P] + shape_of(u), F32)[:]
-            nc.gpsimd.tensor_tensor(out=dst, in0=y_copy[u][:], in1=rel[u][:, which], op=ALU.mult)
-            prod[u, Y, which] = dst
+        def mul_copy(u, which):
+            t = place(f"prod{u}_{Y}_{which}", [P] + shape_of(u), F32)
+            nc.gpsimd.tensor_tensor(out=t[:], in0=y_copy[u][:], in1=rel[u][:, which], op=ALU.mult)
+            prod[u, Y, which] = t[:]
 
         def mul_bank(u, part, which):
             t = place(f"prod{u}_{part}_{which}", [P] + shape_of(u), F32)
             nc.vector.tensor_tensor(out=t[:], in0=heads[u, part][:], in1=rel[u][:, which], op=ALU.mult)
             prod[u, part, which] = t[:]
 
-        def mul_both(u, part):
-            t = place(f"both{u}_{part}", [P, 2] + shape_of(u), F32)
-            nc.vector.tensor_tensor(out=t[:], in0=heads[u, part][:].unsqueeze(1).to_broadcast([P, 2] + shape_of(u)), in1=rel[u], op=ALU.mult)
-            prod[u, part, RR], prod[u, part, RI] = t[:, RR], t[:, RI]
+        def mul_e_both(u):
+            t = place(f"e_both{u}", [P, 2] + shape_of(u), F32)
+            nc.vector.tensor_tensor(out=t[:], in0=heads[u, E][:].unsqueeze(1).to_broadcast([P, 2] + shape_of(u)), in1=rel[u], op=ALU.mult)
+            prod[u, E, RR], prod[u, E, RI] = t[:, RR], t[:, RI]
 
         def sub_z(u, dst):
             nc.gpsimd.tensor_tensor(out=dst, in0=prod[u, Y, RR], in1=prod[u, E, RI], op=ALU.subtract)
 
-        def weave(dst, src):
-            nc.scalar.copy(out=dst.rearrange("p (c i j) -> p c j i", i=4, j=PACK), in_=src.rearrange("p j (c i) -> p c j i", i=4))
+        def interleave(dst, src):
+            nc.scalar.copy(out=dst.rearrange("p (c i j) -> p c j i", i=RUN, j=SLOTS), in_=src.rearrange("p j (c i) -> p c j i", i=RUN))
 
         def add_g(u):
-            acc = psum.tile([P, PACK, P], F32, name=f"turned{u}", tag=TURNED[u])
+            acc = psum.tile([P, SLOTS, P], F32, name=f"turned{u}", tag=TURNED[u])
             for term, src in enumerate((prod[u, Y, RI], prod[u, E, RR])):
-                for n in range(PACK):
+                for n in range(SLOTS):
                     block = src[:, n % 2, (n // 2) * P : (n // 2 + 1) * P] if u < 2 else src[:, n, :]
-                    nc.tensor.matmul(acc[:, n, :], lhsT=block, rhs=ident[:], is_transpose=True, start=(term == 0 and n == 0), stop=(term == 1 and n == PACK - 1))
+                    nc.tensor.matmul(acc[:, n, :], lhsT=block, rhs=ident[:], is_transpose=True, start=(term == 0 and n == 0), stop=(term == 1 and n == SLOTS - 1))
             turned[u] = acc
 
         def round_g(u):
-            pairs[u] = place(f"g_pairs{u}", [P, PACK * P], BF16)
+            pairs[u] = place(f"g_pairs{u}", [P, SLOTS * P], BF16)
             nc.scalar.copy(out=pairs[u][:].rearrange("t (h p e) -> t h p e", h=2, e=2), in_=turned[u][:].rearrange("t (h e) p -> t h p e", e=2))
 
         def turn_g(u, dst):
@@ -190,9 +189,9 @@ def tile_picked_zcplx_soft_p_kernel(tc, x_words, x_scales, w1, w2, rr, ri, p_wor
 
         def combine_last(a):
             walk = "p j (c i) -> p c j i"
-            first, second = ((RR, RI), (RI, RR))[a]
-            nc.vector.tensor_tensor(out=zg3[:, a].rearrange("p (c i j) -> p c j i", i=4, j=PACK), in0=prod[last, Y, first].rearrange(walk, i=4),
-                                    in1=prod[last, E, second].rearrange(walk, i=4), op=(ALU.subtract, ALU.add)[a])
+            with_y, with_e = ((RR, RI), (RI, RR))[a]
+            nc.vector.tensor_tensor(out=zg3[:, a].rearrange("p (c i j) -> p c j i", i=RUN, j=SLOTS), in0=prod[LAST, Y, with_y].rearrange(walk, i=RUN),
+                                    in1=prod[LAST, E, with_e].rearrange(walk, i=RUN), op=(ALU.subtract, ALU.add)[a])
 
         def score(b):
             acc = psum.tile([P, PICKED], F32, name=f"score{b}", tag=SCORES[b])
@@ -204,28 +203,28 @@ def tile_picked_zcplx_soft_p_kernel(tc, x_words, x_scales, w1, w2, rr, ri, p_wor
             bank[b] = acc
 
         def exponentiate(b):
-            m = place(f"nmax{b}", [P, 1], F32)
-            nc.vector.tensor_reduce(out=m[:], in_=bank[b][:], axis=mybir.AxisListType.X, op=ALU.max, negate=True)
+            nmax = place(f"nmax{b}", [P, 1], F32)
+            nc.vector.tensor_reduce(out=nmax[:], in_=bank[b][:], axis=mybir.AxisListType.X, op=ALU.max, negate=True)
             expd[b] = place(f"expd{b}", [P, PICKED], F32)
             total[b] = place(f"total{b}", [P, 1], F32)
-            nc.scalar.activation(out=expd[b][:], in_=bank[b][:], func=ACT.Exp, bias=m[:], scale=1.0, accum_out=total[b][:])
+            nc.scalar.activation(out=expd[b][:], in_=bank[b][:], func=ACT.Exp, bias=nmax[:], scale=1.0, accum_out=total[b][:])
+
+        def invert(b):
+            recip[b] = place(f"recip{b}", [P, 1], F32)
+            nc.vector.reciprocal(out=recip[b][:], in_=total[b][:])
 
         def normalise(b):
-            r = place(f"recip{b}", [P, 1], F32)
-            nc.vector.reciprocal(out=r[:], in_=total[b][:])
             rows = slice(b * P, (b + 1) * P)
-            o = place(f"result{b}", [P, PICKED], F32)
-            if b == 0:
-                nc.gpsimd.tensor_scalar(out=o[:], in0=expd[b][:], scalar1=r[:], scalar2=0.0, op0=ALU.mult, op1=ALU.add)
-                nc.sync.dma_start(out=out[rows, :], in_=o[:])
-            elif b < last:
-                nc.vector.tensor_scalar(out=o[:], in0=expd[b][:], scalar1=r[:], scalar2=None, op0=ALU.mult)
-                nc.sync.dma_start(out=out[rows, :], in_=o[:])
-            else:
-                for h, queue in enumerate((nc.sync, nc.scalar)):
-                    cols = slice(h * HALF, (h + 1) * HALF)
-                    nc.vector.tensor_scalar(out=o[:, cols], in0=expd[b][:, cols], scalar1=r[:], scalar2=None, op0=ALU.mult)
-                    queue.dma_start(out=out[rows, cols], in_=o[:, cols])
+            result = place(f"result{b}", [P, PICKED], F32)
+            width = HALF if b in (0, LAST) else PICKED
+            for c in range(0, PICKED, width):
+                cols = slice(c, c + width)
+                if b == 0:
+                    nc.gpsimd.tensor_scalar(out=result[:, cols], in0=expd[b][:, cols], scalar1=recip[b][:], scalar2=0.0, op0=ALU.mult, op1=ALU.add)
+                else:
+                    nc.vector.tensor_scalar(out=result[:, cols], in0=expd[b][:, cols], scalar1=recip[b][:], scalar2=None, op0=ALU.mult)
+                queue = nc.scalar if b == LAST and c > 0 else nc.sync
+                queue.dma_start(out=out[rows, cols], in_=result[:, cols])
 
         project(0, Y)
         project(0, E)
@@ -240,7 +239,7 @@ def tile_picked_zcplx_soft_p_kernel(tc, x_words, x_scales, w1, w2, rr, ri, p_wor
         project(2, Y)
         project(2, E)
         copy_y(2)
-        z01 = place("z01", [P, PACK, HALF], F32)
+        z01 = place("z01", [P, SLOTS, HALF], F32)
         mul_copy(1, RI)
         sub_z(0, z01[:, :2])
         mul_bank(1, E, RI)
@@ -251,25 +250,26 @@ def tile_picked_zcplx_soft_p_kernel(tc, x_words, x_scales, w1, w2, rr, ri, p_wor
         round_g(0)
         add_g(1)
         round_g(1)
-        project(3, Y)
-        copy_y(3)
+        project(LAST, Y)
+        copy_y(LAST)
         words01 = psum.tile([P, 2, 2, P], F32, name="words01", tag="bank_b")
         turn_g(0, words01[:, :, 0])
         turn_g(1, words01[:, :, 1])
-        project(3, E)
+        project(LAST, E)
         sub_z(1, z01[:, 2:])
-        mul_both(2, E)
-        zg01 = place("zg01", [P, 2, HALF * PACK], BF16)
+        mul_e_both(2)
+        zg01 = place("zg01", [P, 2, HALF * SLOTS], BF16)
         nc.scalar.copy(out=zg01[:, 1].bitcast(F32).rearrange("p (b n h) -> p b n h", b=2, h=2), in_=words01[:].rearrange("p b h n -> p b n h"))
-        weave(zg01[:, 0], z01[:])
+        interleave(zg01[:, 0], z01[:])
+
         p_codes = gather("p_codes", pw_win, tail_t, U32)
         q_codes = gather("q_codes", qw_win, tail_t, U32)
-        mul_bank(3, Y, RI)
-        mul_both(3, E)
+        mul_bank(LAST, Y, RI)
+        mul_e_both(LAST)
         mul_copy(2, RR)
-        mul_copy(3, RR)
-        z_sum2 = place("z_sum2", [P, PACK, P], F32)
-        sub_z(2, z_sum2[:])
+        mul_copy(LAST, RR)
+        z2 = place("z2", [P, SLOTS, P], F32)
+        sub_z(2, z2[:])
         add_g(2)
         round_g(2)
         words2 = psum.tile([P, 2, P], F32, name="words2", tag="bank_d")
@@ -277,20 +277,26 @@ def tile_picked_zcplx_soft_p_kernel(tc, x_words, x_scales, w1, w2, rr, ri, p_wor
         zg_q[0, 0], zg_q[1, 0], zg_q[0, 1], zg_q[1, 1] = quantise("01", zg01[:].rearrange("p a n -> p (a n)"), 4 * P)
         score(0)
         score(1)
-        zg2 = place("zg2", [P, 2, P * PACK], BF16)
+        zg2 = place("zg2", [P, 2, P * SLOTS], BF16)
         nc.scalar.copy(out=zg2[:, 1].bitcast(F32).rearrange("p (n h) -> p n h", h=2), in_=words2[:].rearrange("p h n -> p n h"))
-        weave(zg2[:, 0], z_sum2[:])
-        zg3 = place("zg3", [P, 2, P * PACK], BF16)
+        interleave(zg2[:, 0], z2[:])
+        zg3 = place("zg3", [P, 2, P * SLOTS], BF16)
         combine_last(0)
         combine_last(1)
         exponentiate(0)
         zg_q[2, 0], zg_q[2, 1] = quantise("2", zg2[:].rearrange("p a n -> p (a n)"), 2 * P)
         score(2)
-        zg_q[last, 0], zg_q[last, 1] = quantise("3", zg3[:].rearrange("p a n -> p (a n)"), 2 * P)
-        score(3)
+        zg_q[LAST, 0], zg_q[LAST, 1] = quantise("3", zg3[:].rearrange("p a n -> p (a n)"), 2 * P)
+        score(LAST)
+
         exponentiate(1)
+        invert(0)
         normalise(0)
         exponentiate(2)
-        exponentiate(3)
-        for b in range(1, BLOCKS):
-            normalise(b)
+        exponentiate(LAST)
+        invert(1)
+        invert(2)
+        normalise(1)
+        normalise(2)
+        invert(LAST)
+        normalise(LAST)

from contextlib import ExitStack

import concourse.mybir as mybir
from concourse.masks import make_identity

F32 = mybir.dt.float32
BF16 = mybir.dt.bfloat16
I32 = mybir.dt.int32
U32 = mybir.dt.uint32
U16 = mybir.dt.uint16
U8 = mybir.dt.uint8
FP8X4 = mybir.dt.float8_e4m3fn_x4
ALU = mybir.AluOpType
ACT = mybir.ActivationFunctionType

P = 128
SLOTS = 4
HIDDEN = 512
TABLE = 1024
PICKED = 512
HALF = PICKED // 2
LAST = PICKED // P - 1
SCALE_ROWS = 16
RUN = 4
X_ROW, P_ROW, Q_ROW = 4, 8, 12
RR, RI = 0, 1
Y, E = 0, 1
PIECES = ((0, 2, 0, HALF), (2, 4, 0, HALF), (0, 4, HALF, HALF + P), (0, 4, HALF + P, PICKED))
SHARED = ("g_pairs1", "zg01", "zg3")
TAG = {"dealt1_0": "dealt0_0", "nmax2": "total0"}
TURNED = ("bank_a", "bank_c", "bank_c")
SCORES = ("bank_a", "bank_b", "bank_c", "bank_d")
FLOPS = 4 * 2 * 512 * 512 * 512


def tile_picked_zcplx_soft_p_kernel(tc, x_words, x_scales, w1, w2, rr, ri, p_words, p_scales, q_words, q_scales, offs, tail, out):
    nc = tc.nc
    with ExitStack() as ctx:
        keep = ctx.enter_context(tc.tile_pool(name="keep", bufs=1))
        shared = ctx.enter_context(tc.tile_pool(name="shared", bufs=1))
        psum = ctx.enter_context(tc.psum_pool(name="psum", bufs=1))

        offs_t = keep.tile([P, PICKED // 16], U16, name="offs_t")
        tail_t = keep.tile([P, PICKED // 16], U16, name="tail_t")

        def place(name, shape, dtype):
            if name in SHARED:
                return shared.tile(shape, dtype, name=name, align_bytes=64, offset=0)
            return keep.tile(shape, dtype, name=name, tag=TAG.get(name, name), align_bytes=64)

        def cleared(name, width):
            t = place(name, [P, width], U8)
            nc.gpsimd.memset(t[:].bitcast(I32), 0)
            return t

        def load_scales(window, src):
            nc.sync.dma_start(out=window[:SCALE_ROWS, :].bitcast(I32), in_=src[0].bitcast(I32))

        def spread(plane, rows, first):
            for r in range(4):
                nc.sync.dma_start(out=plane[first + r : P : 32, :].bitcast(I32), in_=rows[r:SCALE_ROWS:4, :].bitcast(I32))

        def load_words(name, src):
            t = place(name, [P, TABLE], I32)
            nc.sync.dma_start(out=t[:], in_=src[0].rearrange("p n t -> p (n t)").bitcast(I32))
            return t

        def load_weight(name, w):
            t = place(name, [P, SLOTS, HIDDEN], F32)
            nc.sync.dma_start(out=t[:], in_=w.rearrange("(p j) c -> p j c", j=SLOTS))
            return t

        def load_relation(which, pair):
            slots = slice(2 * pair, 2 * pair + 2)
            nc.sync.dma_start(out=rel_t[:, which, slots], in_=(rr, ri)[which].rearrange("(p j) c -> p j c", j=SLOTS)[:, slots])

        def gather(name, window, offsets, dtype):
            t = place(name, [P, PICKED], dtype)
            nc.vector.tensor_copy(t[:], window[:].bitcast(dtype).indirect(offsets[:]))
            return t

        def deal(copy, part, pair):
            t = place(f"dealt{part}_{pair}", [P, 2 * P * SLOTS], BF16)
            copy(out=t[:].rearrange("p (t m j) -> p m j t", t=2, j=SLOTS),
                 in_=w_raw[part][:].rearrange("p j (m t) -> p m j t", t=SLOTS)[:, :, :, 2 * pair : 2 * pair + 2])
            dealt[part, pair] = t

        def quantise(name, values, width):
            codes = place("codes" + name, [P, width], U32)
            scales = place("scales" + name, [P, width], U8)
            nc.vector.quantize_mx(out=codes[:].bitcast(FP8X4), scales=scales[:], in_=values)
            return [(codes[:, c : c + P], scales[:, c : c + P]) for c in range(0, width, P)]

        def quantise_weight(part, pair):
            w_q[part, 2 * pair], w_q[part, 2 * pair + 1] = quantise(f"_w{part}_{pair}", dealt[part, pair][:], 2 * P)

        dealt, w_q, heads, y_copy, prod, turned, pairs = {}, {}, {}, {}, {}, {}, {}
        zg_q, bank, expd, total, recip = {}, {}, {}, {}, {}

        xs_win, ps_win, qs_win = (cleared(name, TABLE) for name in ("xs_win", "ps_win", "qs_win"))
        x_plane, p_plane, q_plane = (cleared(name, PICKED) for name in ("x_plane", "p_plane", "q_plane"))
        nc.sync.dma_start(offs_t[:], offs)
        load_scales(xs_win, x_scales)
        xw_win = load_words("xw_win", x_words)
        nc.sync.dma_start(tail_t[:], tail)
        load_scales(ps_win, p_scales)
        load_scales(qs_win, q_scales)
        w_raw = [load_weight("w1_raw", w1), load_weight("w2_raw", w2)]
        x_rows = gather("x_rows", xs_win, offs_t, U8)
        spread(x_plane, x_rows, X_ROW)
        rel_t = place("rel_t", [P, 2, SLOTS, PICKED], F32)
        for pair in range(2):
            load_relation(RI, pair)
            load_relation(RR, pair)
        rel = [rel_t[:, :, j0:j1, c0:c1] for j0, j1, c0, c1 in PIECES]
        pw_win = load_words("pw_win", p_words)
        qw_win = load_words("qw_win", q_words)

        x_codes = gather("x_codes", xw_win, offs_t, U32)
        p_rows = gather("p_rows", ps_win, tail_t, U8)
        q_rows = gather("q_rows", qs_win, tail_t, U8)
        spread(q_plane, q_rows, Q_ROW)
        spread(p_plane, p_rows, P_ROW)
        deal(nc.scalar.copy, Y, 0)
        deal(nc.scalar.copy, Y, 1)
        quantise_weight(Y, 0)
        deal(nc.vector.tensor_copy, E, 0)
        deal(nc.scalar.copy, E, 1)
        quantise_weight(Y, 1)
        quantise_weight(E, 0)
        quantise_weight(E, 1)
        ident = keep.tile([P, P], F32, name="ident")
        make_identity(nc, ident[:])

        def shape_of(u):
            j0, j1, c0, c1 = PIECES[u]
            return [j1 - j0, c1 - c0]

        def project(u, part):
            j0, j1, c0, c1 = PIECES[u]
            acc = psum.tile([P] + shape_of(u), F32, name=f"head{u}_{part}", tag=f"head{part}_{u % 2}")
            for j in range(j0, j1):
                codes, scales = w_q[part, j]
                nc.tensor.matmul_mx(out=acc[:, j - j0, :], lhsT=codes.bitcast(FP8X4), lhsT_scale=scales,
                                    rhs=x_codes[:, c0:c1].bitcast(FP8X4), rhs_scale=x_plane[X_ROW:, c0:c1], start=True, stop=True)
            heads[u, part] = acc

        def copy_y(u):
            y_copy[u] = place(f"y_copy{u}", [P] + shape_of(u), F32)
            nc.scalar.copy(out=y_copy[u][:], in_=heads[u, Y][:])

        def mul_copy(u, which):
            t = place(f"prod{u}_{Y}_{which}", [P] + shape_of(u), F32)
            nc.gpsimd.tensor_tensor(out=t[:], in0=y_copy[u][:], in1=rel[u][:, which], op=ALU.mult)
            prod[u, Y, which] = t[:]

        def mul_bank(u, part, which):
            t = place(f"prod{u}_{part}_{which}", [P] + shape_of(u), F32)
            nc.vector.tensor_tensor(out=t[:], in0=heads[u, part][:], in1=rel[u][:, which], op=ALU.mult)
            prod[u, part, which] = t[:]

        def mul_e_both(u):
            t = place(f"e_both{u}", [P, 2] + shape_of(u), F32)
            nc.vector.tensor_tensor(out=t[:], in0=heads[u, E][:].unsqueeze(1).to_broadcast([P, 2] + shape_of(u)), in1=rel[u], op=ALU.mult)
            prod[u, E, RR], prod[u, E, RI] = t[:, RR], t[:, RI]

        def sub_z(u, dst):
            nc.gpsimd.tensor_tensor(out=dst, in0=prod[u, Y, RR], in1=prod[u, E, RI], op=ALU.subtract)

        def interleave(dst, src):
            nc.scalar.copy(out=dst.rearrange("p (c i j) -> p c j i", i=RUN, j=SLOTS), in_=src.rearrange("p j (c i) -> p c j i", i=RUN))

        def add_g(u):
            acc = psum.tile([P, SLOTS, P], F32, name=f"turned{u}", tag=TURNED[u])
            for term, src in enumerate((prod[u, Y, RI], prod[u, E, RR])):
                for n in range(SLOTS):
                    block = src[:, n % 2, (n // 2) * P : (n // 2 + 1) * P] if u < 2 else src[:, n, :]
                    nc.tensor.matmul(acc[:, n, :], lhsT=block, rhs=ident[:], is_transpose=True, start=(term == 0 and n == 0), stop=(term == 1 and n == SLOTS - 1))
            turned[u] = acc

        def round_g(u):
            pairs[u] = place(f"g_pairs{u}", [P, SLOTS * P], BF16)
            nc.scalar.copy(out=pairs[u][:].rearrange("t (h p e) -> t h p e", h=2, e=2), in_=turned[u][:].rearrange("t (h e) p -> t h p e", e=2))

        def turn_g(u, dst):
            words = pairs[u][:].bitcast(F32)
            for h in range(2):
                nc.tensor.transpose(dst[:, h, :], words[:, h * P : (h + 1) * P], ident[:])

        def combine_last(a):
            walk = "p j (c i) -> p c j i"
            with_y, with_e = ((RR, RI), (RI, RR))[a]
            nc.vector.tensor_tensor(out=zg3[:, a].rearrange("p (c i j) -> p c j i", i=RUN, j=SLOTS), in0=prod[LAST, Y, with_y].rearrange(walk, i=RUN),
                                    in1=prod[LAST, E, with_e].rearrange(walk, i=RUN), op=(ALU.subtract, ALU.add)[a])

        def score(b):
            acc = psum.tile([P, PICKED], F32, name=f"score{b}", tag=SCORES[b])
            tails = ((p_codes[:], p_plane[P_ROW:, :]), (q_codes[:], q_plane[Q_ROW:, :]))
            for a in range(2):
                codes, scales = zg_q[b, a]
                nc.tensor.matmul_mx(out=acc[:], lhsT=codes.bitcast(FP8X4), lhsT_scale=scales,
                                    rhs=tails[a][0].bitcast(FP8X4), rhs_scale=tails[a][1], start=(a == 0), stop=(a == 1))
            bank[b] = acc

        def exponentiate(b):
            nmax = place(f"nmax{b}", [P, 1], F32)
            nc.vector.tensor_reduce(out=nmax[:], in_=bank[b][:], axis=mybir.AxisListType.X, op=ALU.max, negate=True)
            expd[b] = place(f"expd{b}", [P, PICKED], F32)
            total[b] = place(f"total{b}", [P, 1], F32)
            nc.scalar.activation(out=expd[b][:], in_=bank[b][:], func=ACT.Exp, bias=nmax[:], scale=1.0, accum_out=total[b][:])

        def invert(b):
            recip[b] = place(f"recip{b}", [P, 1], F32)
            nc.vector.reciprocal(out=recip[b][:], in_=total[b][:])

        def normalise(b):
            rows = slice(b * P, (b + 1) * P)
            result = place(f"result{b}", [P, PICKED], F32)
            width = HALF if b in (0, LAST) else PICKED
            for c in range(0, PICKED, width):
                cols = slice(c, c + width)
                if b == 0:
                    nc.gpsimd.tensor_scalar(out=result[:, cols], in0=expd[b][:, cols], scalar1=recip[b][:], scalar2=0.0, op0=ALU.mult, op1=ALU.add)
                else:
                    nc.vector.tensor_scalar(out=result[:, cols], in0=expd[b][:, cols], scalar1=recip[b][:], scalar2=None, op0=ALU.mult)
                queue = nc.scalar if b == LAST and c > 0 else nc.sync
                queue.dma_start(out=out[rows, cols], in_=result[:, cols])

        project(0, Y)
        project(0, E)
        project(1, Y)
        project(1, E)
        copy_y(0)
        copy_y(1)
        mul_bank(0, Y, RI)
        mul_bank(0, E, RI)
        mul_copy(0, RR)
        mul_bank(0, E, RR)
        project(2, Y)
        project(2, E)
        copy_y(2)
        z01 = place("z01", [P, SLOTS, HALF], F32)
        mul_copy(1, RI)
        sub_z(0, z01[:, :2])
        mul_bank(1, E, RI)
        mul_bank(2, Y, RI)
        mul_bank(1, E, RR)
        mul_bank(1, Y, RR)
        add_g(0)
        round_g(0)
        add_g(1)
        round_g(1)
        project(LAST, Y)
        copy_y(LAST)
        words01 = psum.tile([P, 2, 2, P], F32, name="words01", tag="bank_b")
        turn_g(0, words01[:, :, 0])
        turn_g(1, words01[:, :, 1])
        project(LAST, E)
        sub_z(1, z01[:, 2:])
        mul_e_both(2)
        zg01 = place("zg01", [P, 2, HALF * SLOTS], BF16)
        nc.scalar.copy(out=zg01[:, 1].bitcast(F32).rearrange("p (b n h) -> p b n h", b=2, h=2), in_=words01[:].rearrange("p b h n -> p b n h"))
        interleave(zg01[:, 0], z01[:])

        p_codes = gather("p_codes", pw_win, tail_t, U32)
        q_codes = gather("q_codes", qw_win, tail_t, U32)
        mul_bank(LAST, Y, RI)
        mul_e_both(LAST)
        mul_copy(2, RR)
        mul_copy(LAST, RR)
        z2 = place("z2", [P, SLOTS, P], F32)
        sub_z(2, z2[:])
        add_g(2)
        round_g(2)
        words2 = psum.tile([P, 2, P], F32, name="words2", tag="bank_d")
        turn_g(2, words2)
        zg_q[0, 0], zg_q[1, 0], zg_q[0, 1], zg_q[1, 1] = quantise("01", zg01[:].rearrange("p a n -> p (a n)"), 4 * P)
        score(0)
        score(1)
        zg2 = place("zg2", [P, 2, P * SLOTS], BF16)
        nc.scalar.copy(out=zg2[:, 1].bitcast(F32).rearrange("p (n h) -> p n h", h=2), in_=words2[:].rearrange("p h n -> p n h"))
        interleave(zg2[:, 0], z2[:])
        zg3 = place("zg3", [P, 2, P * SLOTS], BF16)
        combine_last(0)
        combine_last(1)
        exponentiate(0)
        zg_q[2, 0], zg_q[2, 1] = quantise("2", zg2[:].rearrange("p a n -> p (a n)"), 2 * P)
        score(2)
        zg_q[LAST, 0], zg_q[LAST, 1] = quantise("3", zg3[:].rearrange("p a n -> p (a n)"), 2 * P)
        score(LAST)

        exponentiate(1)
        invert(0)
        normalise(0)
        exponentiate(2)
        exponentiate(LAST)
        invert(1)
        invert(2)
        normalise(1)
        normalise(2)
        invert(LAST)
        normalise(LAST)
